import numpy as np, ml_dtypes
CORES = [40,41,42,43,44,45,46,47]
N = 8
import mx_ref
BF = ml_dtypes.bfloat16
def gentries(a):
    return np.ascontiguousarray(a.reshape(8, 16, -1).transpose(0, 2, 1)).reshape(8, -1)
def gtable(e):
    e = np.asarray(e); return np.ascontiguousarray(e.reshape(8, -1, 16).transpose(0, 2, 1)).reshape(128, -1).astype(np.int32)
def gcols(t, e):
    v = np.concatenate([t.reshape(8, 16, -1, 4), np.zeros((8, 16, 1, 4), BF)], axis=2)
    return np.ascontiguousarray(np.stack([v[g][:, e[g]] for g in range(8)])).reshape(128, -1)
def tile(rs):
    return np.stack(rs, axis=2).reshape(128, -1).astype(BF)
def pick(q, e):
    c = np.concatenate([q[0].reshape(128, -1, 4), np.zeros((128, 1, 4), np.uint8)], axis=1); s = np.concatenate([q[1], np.ones((16, 1), np.uint8)], axis=1)
    return (np.ascontiguousarray(c[:, e].reshape(128, -1)), np.ascontiguousarray(s[:, e]))
def join(*qs):
    return (np.concatenate([q[0] for q in qs], axis=1), np.concatenate([q[1] for q in qs], axis=1))
def put(q, e, v):
    c, s = q[0].reshape(128, -1, 4).copy(), q[1].copy(); c[:, e] = v[0].reshape(128, -1, 4); s[:, e] = v[1]
    return (c.reshape(128, -1), s)
def pk(c, s):
    return (np.ascontiguousarray(c), mx_ref.live(s))
def emit(q):
    return q[0], q[1]
def packed(v, rng):
    q = [mx_ref.quantize(np.ascontiguousarray(v[r])) for r in range(N)]
    return np.stack([a for a, b in q]), np.stack([mx_ref.plane(b, rng) for a, b in q])
def values_of_codes():
    e, c = np.zeros((128, 128, 4), np.float32), np.zeros((128, 2, 4), np.uint8)
    e[np.arange(128), np.arange(128), 0] = 1
    c[:127, :, 0] = np.arange(256).reshape(2, 128).T[:127]
    return mx_ref.matmul(mx_ref.quantize(e.reshape(128, 512).astype(BF)), (c.reshape(128, 8), np.full((16, 2), 127, np.uint8))).T.reshape(-1).astype(np.float64)
CODE_VALUE, SCALE_VALUE = values_of_codes(), 2.0 ** (np.arange(256) - 127.0)
def decode(q):
    return (CODE_VALUE[q[0]].reshape(16, 8, -1, 4) * SCALE_VALUE[q[1]][:, None, :, None] + 0.0).reshape(128, -1).astype(np.float32)
def f(rng, *shape):
    return mx_ref.flush((rng.standard_normal(shape, dtype=np.float32) * np.exp2(rng.integers(-2, 3, shape[:-1] + (1,)))).astype(BF))
def wide(rng, *shape, cols=0):
    v = rng.standard_normal(shape, dtype=np.float32) * np.exp2(rng.integers(-12, 13, shape)).astype(np.float32)
    if cols: v *= np.repeat(np.exp2(rng.integers(-cols, cols + 1, shape[:-2] + (1, shape[-1] // 4))) * (rng.random(shape[:-2] + (1, shape[-1] // 4)) > 0.0625), 4, axis=-1).astype(np.float32)
    return mx_ref.flush(v.astype(BF))
C, H, R = 320, 128, 3
def big(v):
    v = v.astype(np.float32)
    v[np.abs(v) < np.float32(2.0 ** -16)] = 0
    return v.astype(BF)
def numbers_of(rng):
    return {"x": big(f(rng, N, 128, 4 * C)), "u": np.array(f(rng, N, 128, 512)), "v": np.array(f(rng, N, 128, 512))}
def layers(rng, still=[]):
    w = big(f(rng, N, 128, 2048)).reshape(N, 8, 16, 4, 8, 16, 4)
    for i in still: w[:, :, :, :, :, i] = 0
    return w
def weights(rng, w):
    c, s = packed(np.ascontiguousarray(w).reshape(N, 128, 2048), rng)
    return {"wc": c, "ws": s}
def holes(rng):
    return np.sort(np.argsort(rng.random((N, 8, C - 1)), axis=2)[:, :, :H], axis=2)
def throws(rng, a):
    free = np.ones((N, 8, 2 * C), bool)
    free[:, :, C:] = False
    np.put_along_axis(free, a, False, axis=2)
    np.put_along_axis(free, C + np.roll(a, -1, axis=0), True, axis=2)
    e = np.zeros((N, 8, C), np.int64)
    for i in range(C - 1, -1, -1):
        k = (0.5 + rng.random((N, 8, C))) * free[:, :, i:i + C]
        k[:, :, C - 1] = 2.0 * free[:, :, i + C - 1]
        e[:, :, i] = i + np.argmax(k, axis=2)
        np.put_along_axis(free, e[:, :, i:i + 1], False, axis=2)
    return e
def lists(e):
    return np.stack([gtable(e[r]) for r in range(N)])
def meet(rng, e):
    used, out = [False] * C, []
    e = e.tolist()
    for i, k in zip(rng.permutation(C).tolist(), rng.integers(0, 4, C).tolist()):
        j = e[i] + (0, 1, 1 - C, -C)[k]
        if 0 <= j < C and j != i and not used[i] and not used[j]:
            used[i] = used[j] = True
            out += [i, j]
    return np.array(out + [int(i) for i in rng.permutation(C) if not used[i]])
def setup_inputs(rng):
    return {**numbers_of(rng), "p": lists(throws(rng, holes(rng))), **weights(rng, layers(rng))}
def setup_inputs_ties(rng):
    d = numbers_of(rng)
    o = rng.permutation(N)
    x = d["x"].reshape(N, 8, 16, C, 4)
    k = rng.integers(0, 3, (N, 8, C))
    k[o[2]] = 1
    x[:, :, 0] = 0
    x[:, :, 0, :, 0] = k.astype(np.float32).astype(BF)
    u = d["u"].reshape(N, 128, 128, 4)
    u[:, :, ::16] = 0
    for r in range(N):
        for h in range(0, 128, 16): u[r, h, h, 0] = 0.0 if r == o[0] else -1.0 if r == o[1] else 1.0
    return {"x": x.reshape(N, 128, 4 * C), "u": u.reshape(N, 128, 512), "v": d["v"], "p": lists(throws(rng, holes(rng))), **weights(rng, layers(rng, [0]))}
def setup_inputs_near(rng):
    d = numbers_of(rng)
    o = rng.permutation(N) % 4
    low = rng.permutation(8)[:4]
    x = d["x"].astype(np.float32).reshape(N, 8, 16, C, 4)
    u = d["u"].reshape(N, 128, 128, 4)
    x[:, :, 0] = 0
    x[:, :, 8:] = 0
    u[:, :, ::16] = 0
    for r in range(N):
        k = 1.0 if o[r] == 0 else 2.0 ** -30
        if o[r] < 3:
            s = rng.integers(0, 16, (8, C))
            x[r, :, 8] = ((s[:, :, None] >> np.arange(4)) & 1) * np.exp2(np.arange(4) - 23.0)
        else:
            x[r, :, 8, :, 0] = rng.integers(8, 16, (8, C)) * rng.choice([-1.0, 1.0], (8, C)) * 2.0 ** -27
            for g in low: x[r, g, 8:10, :, 0] = rng.integers(8, 15, (2, C)) * 2.0 ** -30
        if o[r] < 2:
            x[r, :, 0, :, 0] = rng.choice([-1.0, 1.0], (8, C))
            x[r, :, 11, :, 0] = 2.0 ** -10
        if o[r] == 2:
            for g in rng.permutation(8)[:4]: x[r, g, 0, rng.integers(C), 0] = 2.0 ** 29
        for h in range(0, 128, 16):
            u[r, h + 8, h] = k
            if o[r] < 2:
                u[r, h, h, 0] = k
                u[r, h + 11, h, 0] = k
            if o[r] == 2: u[r, h, h, 0] = 1.0
            if o[r] == 3 and h // 16 in low: u[r, h + 9, h] = -k
    still = [0, 8, 9, 10, 11, 12, 13, 14, 15]
    w = layers(rng, still)
    w[:, :, still] = 0
    return {"x": x.reshape(N, 128, 4 * C).astype(BF), "u": u.reshape(N, 128, 512), "v": d["v"], "p": lists(throws(rng, holes(rng))), **weights(rng, w)}
def setup_inputs_huge(rng):
    d = numbers_of(rng)
    h, o = rng.permutation(8), rng.permutation(N)
    c = rng.choice([-1.0, 1.0], (N, 1, 1, C, 1))
    c[o == 0] = 1.0
    x = (0.9 + 0.1 * rng.random((N, 8, 16, C, 4))) * 2.0 ** 30
    x[:, h[4:]] *= c
    a = (0.9 + 0.1 * rng.random((N, 8, 16, 8, 4))) * 2.0 ** 30
    for r in range(N):
        if o[r] == 0: a[r] *= -1.0
        elif o[r] % 2 == 1:
            a[r] *= -1.0
            a[r, h[4:]] = 0
        else: a[r, h[:4]] = 0
    u = d["u"].reshape(N, 128, 128, 4)
    u[:, :, ::16] = a.reshape(N, 128, 8, 4).astype(np.float32).astype(BF)
    w = np.zeros((N, 128, 4, 128, 4), np.float32)
    i = np.arange(128)
    for b in range(4): w[:, i, b, i, b] = -1
    return {"x": x.astype(np.float32).reshape(N, 128, 4 * C).astype(BF), "u": u.reshape(N, 128, 512), "v": d["v"], "p": lists(throws(rng, holes(rng))), **weights(rng, w.astype(BF))}
def setup_inputs_edges(rng):
    d = numbers_of(rng)
    h, a = rng.permutation(8), holes(rng)
    a[:, h[:2]] = np.arange(H)
    a[:, h[2:4]] = np.arange(C - 1 - H, C - 1)
    e = throws(rng, a)
    e[:, h[:2]] = np.arange(C) + H
    x = d["x"].reshape(N, 8, 16, C, 4)
    x[:, :, :3] = 0
    for r in range(N):
        for g in range(8):
            n = np.zeros(C, np.int64)
            n[meet(rng, e[r, g])] = np.arange(C - 1, -1, -1)
            for i in range(3): x[r, g, i, :, 0] = ((n >> (6 - 3 * i)) & 7).astype(np.float32).astype(BF)
    k = np.exp2(rng.integers(-2, 3, (N, 8, 1, C, 1)))
    b = (2 * rng.integers(0, 8, (N, 8, 8, C, 4)) + 1) * 2.0 ** -16 * k
    b[:, :, 0, :, 0] = 1.96875 * k[:, :, 0, :, 0]
    b *= rng.choice([-1.0, 1.0], b.shape)
    x[:, :, 8:] = b.astype(np.float32).astype(BF)
    u = d["u"].reshape(N, 128, 128, 4)
    u[:, :, ::16] = 0
    for g in range(0, 128, 16):
        for i in range(3): u[:, g + i, g, 0] = 2.0 ** (6 - 3 * i)
    return {"x": x.reshape(N, 128, 4 * C), "u": u.reshape(N, 128, 512), "v": d["v"], "p": lists(e), **weights(rng, layers(rng, [0, 1, 2, 8, 9, 10, 11, 12, 13, 14, 15]))}
def setup_inputs_spread(rng):
    d = setup_inputs(rng)
    d["x"] = big(wide(rng, N, 128, 4 * C, cols=6))
    return d
def check_inputs(d):
    b = []
    for k in ("x", "u", "v"):
        a = np.abs(d[k].astype(np.float32))
        if not (np.isfinite(a).all() and ((a == 0) | (a >= 2.0 ** -30) & (a <= 2.0 ** 30)).all()): b.append("a value of " + k)
    e = np.stack([gentries(d["p"][r]) for r in range(N)]).astype(np.int64)
    t, s = e - np.arange(C), np.sort(e, axis=2)
    if ((t < 0) | (t >= C)).any(): b.append("p: a landing out of its column's bounds")
    if (s[:, :, 1:] == s[:, :, :-1]).any(): b.append("p: equal landings")
    if (np.count_nonzero(e >= C, axis=2) != H).any(): b.append("p: the number of crossing landings")
    k = np.concatenate([s[:, :, :C - H], np.roll(s[:, :, C - H:], 1, axis=0) - C], axis=2)
    if (np.sort(k, axis=2) != np.arange(C)).any(): b.append("p: crossing landings aren't the next rank's holes")
    none, least, most = [emit(mx_ref.quantize(np.full((128, 16), k, np.float32).astype(BF)))[1][0, 0] for k in (0.0, 2.0 ** -30, 2.0 ** 30)]
    for r in range(N):
        if ((d["wc"][r] == 0x7F) | (d["wc"][r] == 0xFF)).any(): b.append("wc: a code that is no number")
        s = mx_ref.live(d["ws"][r])
        if ((s != none) & ((s < least) | (s > most))).any(): b.append("ws: a scale out of range")
    return b
def reference(x, u, v, p, wc, ws):
    qu = [mx_ref.quantize(u[r]) for r in range(N)]
    lay = [pk(wc[r], ws[r]) for r in range(N)]
    now = [x[r] for r in range(N)]
    land = np.stack([gentries(p[r]) for r in range(N)]).astype(np.int64)
    for t in range(R):
        for r in range(N):
            s = mx_ref.matmul(qu[r], mx_ref.quantize(now[r]))[::16] + np.float32(0.0)
            o = np.argsort(-s, axis=1, kind="stable")
            a, b = o[:, ::2], o[:, 1::2]
            la, lb = np.take_along_axis(land[r], a, axis=1), np.take_along_axis(land[r], b, axis=1)
            ok = (a <= lb) & (lb < a + C) & (b <= la) & (la < b + C)
            np.put_along_axis(land[r], a, np.where(ok, lb, la), axis=1)
            np.put_along_axis(land[r], b, np.where(ok, la, lb), axis=1)
        back, hits = np.argsort(land, axis=2), np.sort(land, axis=2)
        given = [mx_ref.quantize(gcols(now[r], back[r][:, C - H:])) for r in range(N)]
        new = []
        for r in range(N):
            both = np.concatenate([now[r], decode(given[r - 1]).astype(BF)], axis=1)
            e = np.zeros((8, C), np.int64)
            np.put_along_axis(e, hits[r][:, :C - H], back[r][:, :C - H], axis=1)
            np.put_along_axis(e, hits[r - 1][:, C - H:] - C, np.stack([C + np.arange(H)] * 8), axis=1)
            z = ((gcols(both, e).astype(np.float32) + now[r].astype(np.float32)) * np.float32(0.5)).astype(BF)
            q = mx_ref.quantize(z)
            new.append(tile([mx_ref.matmul(pick(lay[r], np.arange(128 * b, 128 * b + 128)), q) * np.float32(0.03125) + z[:, b::4].astype(np.float32) for b in range(4)]))
        now = new
    y, ol = np.zeros((N, 128, C), np.float32), np.zeros((N, 8, C), np.float32)
    oc, osc = np.zeros((N, 128, 4 * C), np.uint8), np.zeros((N, 16, C), np.uint8)
    for r in range(N):
        q = mx_ref.quantize(now[r])
        y[r] = mx_ref.matmul(mx_ref.quantize(v[r]), q)
        ol[r] = land[r]
        oc[r], osc[r] = emit(q)
    return {"y": y, "ol": ol, "oc": oc, "osc": osc}

@@ -1,0 +1,297 @@
+from concourse.mybir import dt, AluOpType, ActivationFunctionType
+
+A = AluOpType
+COPY = ActivationFunctionType.Copy
+C, ROUNDS = 320, 3
+NC = C // 16
+F8 = "float8_e4m3fn_x4"
+
+SCRATCH = {}
+
+
+def _declare(names, columns, dtype, where="sbuf"):
+    for name in names.split():
+        SCRATCH[name] = (where, [128, columns], dtype)
+
+
+_declare("xt0 xt1 z z32 uu hx", 4 * C, "bfloat16")
+_declare("ut vt", 512, "bfloat16")
+_declare("eo ee", 516, "bfloat16")
+_declare("hw", 8 * C, "bfloat16")
+_declare("fb", NC * C, "bfloat16")
+_declare("te ts kk", C, "bfloat16")
+_declare("uq uqr vq", 128, F8)
+_declare("us usr vs", 128, "uint8")
+_declare("wq eq", 512, F8)
+_declare("wp es", 512, "uint8")
+_declare("zq qx0 qx1 qx2 qx3 qp0 qp1 qp2", C, F8)
+_declare("zs sx0 sx1 sx2 sx3 sp0 sp1 sp2", C, "uint8")
+_declare("nb gb", C + 32, "float32")
+_declare("wb", 3 * C, "float32")
+_declare("tt", 2 * C + 32, "float32")
+_declare("ex vb wo j16 iof iog yb olb l50 l51 l52", C, "float32")
+_declare("w1 w2 sw", 24, "float32")
+_declare("acc alt pxi dl mm md db pm pf ef ci iw pbf lw0 lw1 lw2 lw3", NC, "float32")
+_declare("xx cl ok ka", 2 * NC, "float32")
+_declare("qf q20 me mo", 1, "float32")
+_declare("pli par pv pin", NC, "int32")
+_declare("bl", 2 * NC, "int32")
+_declare("pb", C, "int32")
+_declare("c8", 8, "int32")
+_declare("pi qi oi", 1, "int32")
+_declare("plu pxu pu eu exl pbl lu0 lu1 lu2 la0 la1 la2", NC, "uint16")
+_declare("ul", 8, "uint16")
+_declare("ps0 ps1 ps2 ps3 ps4 ps5 ps6 ps7", 512, "float32", "psum")
+
+SEMAPHORES = (["v", "a", "t", "gc_", "dx", "du", "dp", "dpb", "dw", "dv", "dy", "dol", "doc"]
+              + ["%s%d" % (n, t) for n in ("rq", "rl", "lq", "ll") for t in range(ROUNDS)])
+
+
+def rank_program(g, core, T, topo):
+    rank = T.rank_of(core)
+    if rank is None:
+        return
+    nxt = T.cores[(rank + 1) % len(T.cores)]
+    rid, pid = topo.addr(nxt)[:2]
+    mask = topo.mask(core, nxt)
+    nmask = len(topo.engines(core, nxt))
+    eng = {"v": g.vector, "a": g.scalar, "t": g.tensor, "gc_": g, "s": g.sync}
+
+    count, known, snap = {}, {q: {} for q in eng}, {}
+    wrote, read, order = {}, {}, [0]
+
+    def need(q, toks):
+        for k in sorted(set(toks), key=lambda k: (snap.get(k, (0, {}))[0], k), reverse=True):
+            if known[q].get(k[0], 0) >= k[1]:
+                continue
+            eng[q].wait_ge(T.sem[k[0]], k[1])
+            for s, m in list(snap.get(k, (0, {}))[1].items()) + [k]:
+                if known[q].get(s, 0) < m:
+                    known[q][s] = m
+
+    def deps(q, reads, writes):
+        toks = []
+        for k in reads:
+            if k in wrote:
+                toks.append(wrote[k])
+            if k[:2] == "ps":
+                toks += [(s, m) for s, m in read.get(k, {}).items() if s != q]
+        for k in writes:
+            if k in wrote:
+                toks.append(wrote[k])
+            toks += [(s, m) for s, m in read.get(k, {}).items() if s != q]
+        return toks
+
+    def note(tok, reads, writes, q):
+        order[0] += 1
+        snap[tok] = (order[0], dict(known[q]))
+        for k in reads:
+            read.setdefault(k, {})[tok[0]] = tok[1]
+        for k in writes:
+            wrote[k] = tok
+            read[k] = {}
+
+    def op(q, fn, reads, writes):
+        need(q, deps(q, reads, writes))
+        fn().then_inc(T.sem[q], 1)
+        count[q] = count.get(q, 0) + 1
+        note((q, count[q]), reads, writes, q)
+
+    def dma(q, out, in_, sem, reads, writes):
+        need(q, deps(q, reads, writes))
+        eng[q].dma_start(out, in_).then_inc(T.sem[sem], 16)
+        count[sem] = count.get(sem, 0) + 16
+        note((sem, count[sem]), reads, writes, q)
+
+    def send(out, in_, rsem, lsem, reads):
+        need("gc_", deps("gc_", reads, []))
+        g.remote_dma(out, in_, T.sem[rsem], T.sem[lsem], pid, rid, mask)
+        count[lsem] = count.get(lsem, 0) + nmask
+
+    V, S, P = g.vector, g.scalar, g.tensor
+
+    def tt(out, a, b, o, reads, writes):
+        op("v", lambda: V.tensor_tensor(out, a, b, o), reads, writes)
+
+    def ts(out, a, s1, s2, o, reads, writes):
+        if len(o) == 1:
+            op("v", lambda: V.tensor_scalar(out, a, s1, None, o[0]), reads, writes)
+        else:
+            op("v", lambda: V.tensor_scalar(out, a, s1, s2, o[0], o[1]), reads, writes)
+
+    def cp(out, a, reads, writes):
+        op("v", lambda: V.tensor_copy(out, a), reads, writes)
+
+    def act(out, a, reads, writes, scale=1.0, accum=None):
+        op("a", lambda: S.activation(out, a, COPY, scale=scale, accum_out=accum), reads, writes)
+
+    def quant(q, s, a, reads, writes):
+        op("v", lambda: V.quantize_mx(q, s, a), reads, writes)
+
+    def mm(out, lq, ls, rq, rs, reads, writes):
+        op("t", lambda: P.matmul_mx(out, lq, ls, rq, rs, True, True), reads, writes)
+
+    for t in range(ROUNDS):
+        wrote["qp%d" % t] = ("rq%d" % t, 2 * nmask)
+        wrote["la%d" % t] = ("rl%d" % t, nmask)
+
+    dma("s", T.xt0[:], T.x[:], "dx", [], ["xt"])
+    dma("a", T.ut[:], T.u[:], "du", [], ["ut"])
+    dma("a", T.pin[:], T.p[:], "dp", [], ["pin"])
+    for r in range(16):
+        dma("s", T.pb[r:128:16, :], T.p[:], "dpb", [], [])
+    wrote["pb"] = ("dpb", count["dpb"])
+    dma("s", T.wq[:].bitcast(dt.uint8), T.wc[:], "dw", [], [])
+    dma("s", T.wp[:], T.ws[:], "dw", [], ["w"])
+    dma("s", T.vt[:], T.v[:], "dv", [], ["vt"])
+
+    def iota(out, pattern, mul, key):
+        op("gc_", lambda: g.iota(out, pattern, 0, mul, allow_small_or_imprecise_dtypes=True), [], [key])
+
+    op("v", lambda: V.memset(T.eo[:], 1.0), [], ["eo"])
+    for name, k in (("nb", 0), ("nb", C + 16), ("gb", 0), ("gb", C + 16), ("wb", C - 16), ("wb", 2 * C)):
+        op("v", lambda: V.memset(T[name][:, k:k + 16], 0.0), [], [name + "_pad"])
+    wrote["wb"] = wrote["wb_pad"]
+    iota(T.c8[:], [[16, 8]], 0, "c8")
+    iota(T.pi[:], [[1, 1]], 1, "pi")
+    iota(T.ci[:], [[1, NC]], 0, "ci")
+    iota(T.j16[:], [[0, NC], [1, 16]], 0, "j16")
+    op("gc_", lambda: g.affine_select(T.ee[:], T.eo[:], [[1, 516]], A.is_equal, 0.0, -3, -4), ["eo"], ["ee"])
+    iota(T.iof[:], [[1, C]], 0, "iof")
+    cp(T.ul[:], T.c8[:], ["c8"], ["ul"])
+    ts(T.qi[:], T.pi[:], 15, None, [A.bitwise_and], ["pi"], ["qi"])
+    ts(T.oi[:], T.pi[:], 16, None, [A.bitwise_and], ["pi"], ["oi"])
+    cp(T.qf[:], T.qi[:], ["qi"], ["qf"])
+    ts(T.me[:], T.oi[:], 0.0, None, [A.is_equal], ["oi"], ["me"])
+    ts(T.mo[:], T.oi[:], 0.0, None, [A.is_gt], ["oi"], ["mo"])
+    ts(T.q20[:], T.qf[:], 20.0, None, [A.mult], ["qf"], ["q20"])
+    cp(T.exl[:], T.ci[:], ["ci"], ["exl"])
+    ts(T.iw[:], T.ci[:], 16.0, T.qf[:, 0:1], [A.mult, A.add], ["ci", "qf"], ["iw"])
+    cp(T.ka[:, 0:NC], T.iw[:], ["iw"], ["kaw"])
+    ts(T.pbf[:], T.ci[:], T.q20[:, 0:1], None, [A.add], ["ci", "q20"], ["pbf"])
+    cp(T.pbl[:], T.pbf[:], ["pbf"], ["pbl"])
+    ts(T.kk[:], T.j16[:], T.qf[:, 0:1], None, [A.is_gt], ["j16", "qf"], ["kk"])
+
+    quant(T.uq[:], T.us[:], T.ut[:], ["ut"], ["uq"])
+    op("v", lambda: V.tensor_copy(T.uqr[:, 0:128].bitcast(dt.uint32), T.uq[:, 0:128].bitcast(dt.uint32).indirect(T.ul[:, 0:8])), ["uq", "ul"], ["uqr"])
+    op("v", lambda: V.tensor_copy(T.usr[:, 0:128], T.us[:, 0:128].indirect(T.ul[:, 0:8])), ["uq", "ul"], ["usr"])
+    for b in range(4):
+        quant(T.eq[:, 128 * b:128 * b + 128], T.es[:, 128 * b:128 * b + 128], T.ee[:, 3 - b:515 - b], ["ee"], ["eq%d" % b])
+
+    def to_wrapped(buf, a, out, bkeys, okey, bank=None, bank_key=None):
+        if bank is None:
+            op("v", lambda: V.transpose(T.tt[:, 0:C], buf[:, a:a + C]), bkeys, ["tta"])
+        else:
+            op("v", lambda: V.transpose(T.tt[:, 0:C], bank[:, 0:C]), [bank_key], ["tta"])
+        op("v", lambda: V.transpose(T.tt[:, C:2 * C + 32], buf[:, a - 16:a + C + 16]), bkeys, ["ttb"])
+        e = 2 * C + 32
+        ts(T.w1[:, 0:21], T.tt[:, 0:e:32], T.me[:, 0:1], None, [A.mult], ["tta", "ttb", "me"], ["w1"])
+        ts(T.w2[:, 0:21], T.tt[:, 16:e:32], T.mo[:, 0:1], None, [A.mult], ["tta", "ttb", "mo"], ["w2"])
+        tt(out[:, 0:NC:2], T.w1[:, 0:10], T.w2[:, 10:20], A.add, ["w1", "w2"], [okey + "_even"])
+        tt(out[:, 1:NC:2], T.w1[:, 11:21], T.w2[:, 0:10], A.add, ["w1", "w2"], [okey + "_odd"])
+
+    for t in range(ROUNDS):
+        xt = T.xt0 if t == 0 else T.xt1
+        xk = ["xt"] if t == 0 else ["x%d" % b for b in range(4)]
+        qx, sx, qk = T["qx%d" % t], T["sx%d" % t], "qx%d" % t
+        quant(qx[:], sx[:], xt[:], xk, [qk])
+        mm(T.ps5[:, 0:C], T.uqr[:], T.usr[:], qx[:], sx[:], ["uqr", "usr", qk], ["ps5"])
+        mm(T.ps0[:, 0:C], T.uqr[:], T.usr[:], qx[:], sx[:], ["uqr", "usr", qk], ["ps0"])
+        send(T["qp%d" % t][:].bitcast(dt.uint8), qx[:].bitcast(dt.uint8), "rq%d" % t, "lq%d" % t, [qk])
+        send(T["sp%d" % t][:], sx[:], "rq%d" % t, "lq%d" % t, [qk])
+        act(T.nb[:, 16:16 + C], T.ps5[:, 0:C], ["ps5"], ["nb"])
+        to_wrapped(T.nb, 16, T.sw, ["nb", "nb_pad"], "sw", T.ps0, "ps0")
+        sk = ["sw_even", "sw_odd"]
+        for c in range(NC):
+            f, e, sc = C * c, 16 * c + 16, T.sw[:, c:c + 1]
+            fk = ["fl%d" % c, "fh%d" % c]
+            ts(T.fb[:, f:f + e], T.nb[:, 16:16 + e], sc, None, [A.is_ge], ["nb"] + sk, fk[:1])
+            if e < C:
+                ts(T.fb[:, f + e:f + C], T.nb[:, 16 + e:16 + C], sc, None, [A.is_gt], ["nb"] + sk, fk[1:])
+            act(T.fb[:, f:f + C], T.fb[:, f:f + C], fk, fk + ["acc"], accum=T.acc[:, c:c + 1])
+            if c == 6:
+                act(T.ex[:], T.sw[:, 0:NC].indirect(T.exl[:]), sk + ["exl"], ["ex"])
+            if c == 8 and t == 0:
+                ts(T.l50[:], T.pb[:].indirect(T.pbl[:]), 512.0, None, [A.mult], ["pb", "pbl"], ["l50"])
+                cp(T.lw0[:], T.pin[:], ["pin"], ["lw0"])
+                ts(T.iog[:], T.iof[:], float(C), None, [A.add], ["iof"], ["iog"])
+                tt(T.vb[:], T.l50[:], T.iof[:], A.add, ["l50", "iof"], ["vb"])
+        lw, ln, lk = T["lw%d" % t], T["lw%d" % (t + 1)], "lw%d" % t
+        ts(T.ka[:, NC:2 * NC], lw[:], float(1 - C), None, [A.add], [lk], ["kal"])
+        tt(T.te[:], T.ps0[:, 0:C], T.ex[:], A.is_equal, ["ps0", "ex"], ["te"])
+        op("v", lambda: V.tensor_tensor_scan(T.ts[:], T.te[:], T.kk[:], 0.0, A.add, A.mult), ["te", "kk"], ["ts"])
+        for dst, w, key in ((T.hw, 2 * C, "h"), (T.hx, C, "g")):
+            for b in range(4):
+                if t == 0:
+                    act(dst[:, w * b:w * b + C], T.xt0[:, b:4 * C:4], ["xt"], [key + str(b)], scale=0.5)
+                else:
+                    act(dst[:, w * b:w * b + C], T.uu[:, C * b:C * b + C], ["uu%d" % b], [key + str(b)], scale=2.0 ** -6)
+        for b in range(4):
+            k = "ps%d" % (1 + b)
+            mm(T[k][:, 0:C], T.eq[:, 128 * b:128 * b + 128], T.es[:, 128 * b:128 * b + 128], T["qp%d" % t][:], T["sp%d" % t][:], ["eq%d" % b, "qp%d" % t], [k])
+            act(T.hw[:, 2 * C * b + C:2 * C * b + 2 * C], T[k][:, 0:C], [k], ["d%d" % b], scale=0.5)
+        tt(T.pli[:], T.acc[:], T.ts[:, 15:C:16], A.subtract, ["acc", "ts"], ["pli"])
+        ts(T.plu[:], T.pli[:], -1.0, None, [A.add], ["pli"], ["plu"])
+        ts(T.par[:], T.pli[:], 1, None, [A.bitwise_and], ["pli"], ["par"])
+        op("v", lambda: V.tensor_copy(T.wo[:, 0:C].indirect(T.plu[:]), T.vb[:]), ["plu", "vb"], ["wo"])
+        ts(T.alt[:], T.par[:], 2.0, -2.0, [A.mult, A.add], ["par"], ["alt"])
+        tt(T.pxi[:], T.pli[:], T.alt[:], A.add, ["pli", "alt"], ["pxi"])
+        cp(T.pxu[:], T.pxi[:], ["pxi"], ["pxu"])
+        cp(T.gb[:, 16:16 + C], T.wo[:, 0:C].indirect(T.pxu[:]), ["wo", "pxu"], ["gb"])
+        to_wrapped(T.gb, 16, T.pv, ["gb", "gb_pad"], "pv")
+        pk = ["pv_even", "pv_odd"]
+        lb, bi = T.bl[:, 0:NC], T.bl[:, NC:2 * NC]
+        ts(lb, T.pv[:], 9, None, [A.arith_shift_right], pk, ["lb"])
+        ts(bi, T.pv[:], 511, None, [A.bitwise_and], pk, ["bi"])
+        tt(T.xx[:], T.bl[:], T.ka[:], A.subtract, ["lb", "bi", "kaw", "kal"], ["xx"])
+        tt(T.dl[:], lb, lw[:], A.subtract, ["lb", lk], ["dl"])
+        ts(T.cl[:], T.xx[:], 0.0, float(C - 1), [A.max, A.min], ["xx"], ["cl"])
+        tt(T.ok[:], T.cl[:], T.xx[:], A.is_equal, ["cl", "xx"], ["ok"])
+        tt(T.mm[:], T.ok[:, 0:NC], T.ok[:, NC:2 * NC], A.mult, ["ok"], ["mm"])
+        tt(T.md[:], T.mm[:], T.dl[:], A.mult, ["mm", "dl"], ["md"])
+        tt(ln[:], lw[:], T.md[:], A.add, [lk, "md"], ["lw%d" % (t + 1)])
+        lu, uk = T["lu%d" % t], "lu%d" % t
+        cp(lu[:], ln[:], ["lw%d" % (t + 1)], [uk])
+        send(T["la%d" % t][:], lu[:], "rl%d" % t, "ll%d" % t, [uk])
+        cp(T.wb[:, C:3 * C].indirect(lu[:]), T.iof[:], [uk, "iof"], ["wb"])
+        tt(T.db[:], bi, T.iw[:], A.subtract, ["bi", "iw"], ["db"])
+        tt(T.pm[:], T.mm[:], T.db[:], A.mult, ["mm", "db"], ["pm"])
+        tt(T.pf[:], T.pm[:], T.iw[:], A.add, ["pm", "iw"], ["pf"])
+        cp(T.pu[:], T.pf[:], ["pf"], ["pu"])
+        l5, l5k = T["l5%d" % t], "l5%d" % t
+        if t + 1 < ROUNDS:
+            act(T["l5%d" % (t + 1)][:], l5[:].indirect(T.pu[:]), [l5k, "pu"], ["l5%d" % (t + 1)])
+            tt(T.vb[:], l5[:].indirect(T.pu[:]), T.iof[:], A.add, [l5k, "pu", "iof"], ["vb"])
+        else:
+            act(T.olb[:], l5[:].indirect(T.pu[:]), [l5k, "pu"], ["olb"], scale=2.0 ** -9)
+            dma("s", T.ol[:], T.olb[0:128:16, :], "dol", ["olb"], [])
+            quant(T.vq[:], T.vs[:], T.vt[:], ["vt"], ["vq"])
+        cp(T.wb[:, 0:2 * C].indirect(T["la%d" % t][:]), T.iog[:], ["la%d" % t, "iog"], ["wb"])
+        to_wrapped(T.wb, C, T.ef, ["wb"], "ef")
+        cp(T.eu[:], T.ef[:], ["ef_even", "ef_odd"], ["eu"])
+        for b in range(4):
+            o = 2 * C * b
+            tt(T.z[:, b:4 * C:4], T.hw[:, o:o + 2 * C].indirect(T.eu[:]), T.hx[:, C * b:C * b + C], A.add, ["eu", "h%d" % b, "g%d" % b, "d%d" % b], ["z%d" % b])
+            act(T.z32[:, C * b:C * b + C], T.z[:, b:4 * C:4], ["z%d" % b], ["zz%d" % b], scale=32.0)
+        quant(T.zq[:], T.zs[:], T.z[:], ["z%d" % b for b in range(4)], ["zq"])
+        for b in range(4):
+            k = ("ps5", "ps6", "ps7", "ps1")[b]
+            u = T.uu[:, C * b:C * b + C]
+            mm(T[k][:, 0:C], T.wq[:, 128 * b:128 * b + 128], T.wp[:, 128 * b:128 * b + 128], T.zq[:], T.zs[:], ["w", "zq"], [k])
+            tt(u, T[k][:, 0:C], T.z32[:, C * b:C * b + C], A.add, [k, "zz%d" % b], ["uu%d" % b])
+            if b < 3:
+                act(T.xt1[:, b:4 * C:4], u, ["uu%d" % b], ["x%d" % b], scale=2.0 ** -5)
+            else:
+                ts(T.xt1[:, b:4 * C:4], u, 2.0 ** -5, None, [A.mult], ["uu%d" % b], ["x%d" % b])
+
+    q3, s3 = T["qx%d" % ROUNDS], T["sx%d" % ROUNDS]
+    quant(q3[:], s3[:], T.xt1[:], ["x%d" % b for b in range(4)], ["q3"])
+    mm(T.ps0[:, 0:C], T.vq[:], T.vs[:], q3[:], s3[:], ["vq", "q3"], ["ps0"])
+    dma("s", T.oc[:], q3[:].bitcast(dt.uint8), "doc", ["q3"], [])
+    for k in range(4):
+        dma("s", T.osc[4 * k:4 * k + 4, :], s3[32 * k:32 * k + 4, :], "doc", ["q3"], [])
+    act(T.yb[:], T.ps0[:, 0:C], ["ps0"], ["yb"])
+    dma("a", T.y[:], T.yb[:], "dy", ["yb"], [])
+    for t in range(ROUNDS):
+        count["rq%d" % t], count["rl%d" % t] = 2 * nmask, nmask
+    need("s", [(s, m) for s, m in count.items()])

@@ -1,9 +1,11 @@
-from concourse.mybir import dt, AluOpType, ActivationFunctionType
+from concourse.mybir import dt, AluOpType, ActivationFunctionType, AxisListType
 
 A = AluOpType
 COPY = ActivationFunctionType.Copy
 C, ROUNDS = 320, 3
+E = C + 32
 NC = C // 16
+ON_VECTOR = (NC - 1,)
 F8 = "float8_e4m3fn_x4"
 
 SCRATCH = {}
@@ -14,7 +16,8 @@ def _declare(names, columns, dtype, where="sbuf"):
         SCRATCH[name] = (where, [128, columns], dtype)
 
 
-_declare("xt0 xt1 z z32 uu hx", 4 * C, "bfloat16")
+_declare("xt0 xt1", 4 * E, "bfloat16")
+_declare("z z32 uu hx", 4 * C, "bfloat16")
 _declare("ut vt", 512, "bfloat16")
 _declare("eo ee", 516, "bfloat16")
 _declare("hw", 8 * C, "bfloat16")
@@ -24,23 +27,28 @@ _declare("uq uqr vq", 128, F8)
 _declare("us usr vs", 128, "uint8")
 _declare("wq eq", 512, F8)
 _declare("wp es", 512, "uint8")
-_declare("zq qx0 qx1 qx2 qx3 qp0 qp1 qp2", C, F8)
-_declare("zs sx0 sx1 sx2 sx3 sp0 sp1 sp2", C, "uint8")
-_declare("nb gb", C + 32, "float32")
+_declare("zq qx3 qp0 qp1 qp2", C, F8)
+_declare("zs sx3 sp0 sp1 sp2", C, "uint8")
+_declare("qx0 qx1 qx2", E, F8)
+_declare("sx0 sx1 sx2", E, "uint8")
+_declare("gb", E, "float32")
 _declare("wb", 3 * C, "float32")
-_declare("tt", 2 * C + 32, "float32")
-_declare("ex vb wo j16 iof iog yb olb l50 l51 l52", C, "float32")
-_declare("w1 w2 sw", 24, "float32")
-_declare("acc alt pxi dl mm md db pm pf ef ci iw pbf lw0 lw1 lw2 lw3", NC, "float32")
+_declare("tt", C + E, "float32")
+_declare("nb ex vb wo j16 iof iog yb olb l50 l51 l52", C, "float32")
+_declare("sw", 32, "float32")
+_declare("acc alt pxi dl mm md db pm pf ci iw pbf lw0 lw1 lw2 lw3", NC, "float32")
 _declare("xx cl ok ka", 2 * NC, "float32")
-_declare("qf q20 me mo", 1, "float32")
-_declare("pli par pv pin", NC, "int32")
+_declare("qf q20 k1 k2 k3", 1, "float32")
+_declare("pli par pin", NC, "int32")
+_declare("pv", 32, "int32")
 _declare("bl", 2 * NC, "int32")
 _declare("pb", C, "int32")
 _declare("c8", 8, "int32")
-_declare("pi qi oi", 1, "int32")
-_declare("plu pxu pu eu exl pbl lu0 lu1 lu2 la0 la1 la2", NC, "uint16")
+_declare("pi qi oi si ri", 1, "int32")
+_declare("plu pxu pu exl pbl lu0 lu1 lu2 la0 la1 la2", NC, "uint16")
+_declare("eu", 32, "uint16")
 _declare("ul", 8, "uint16")
+_declare("wl", 2, "uint16")
 _declare("ps0 ps1 ps2 ps3 ps4 ps5 ps6 ps7", 512, "float32", "psum")
 
 SEMAPHORES = (["v", "a", "t", "gc_", "dx", "du", "dp", "dpb", "dw", "dv", "dy", "dol", "doc"]
@@ -135,41 +143,49 @@ def rank_program(g, core, T, topo):
         wrote["qp%d" % t] = ("rq%d" % t, 2 * nmask)
         wrote["la%d" % t] = ("rl%d" % t, nmask)
 
-    dma("s", T.xt0[:], T.x[:], "dx", [], ["xt"])
+    lo, hi = 4 * 16, 4 * (16 + C)
+    dma("s", T.xt0[:, lo:hi], T.x[:], "dx", [], [])
     dma("a", T.ut[:], T.u[:], "du", [], ["ut"])
-    dma("a", T.pin[:], T.p[:], "dp", [], ["pin"])
+    dma("s", T.xt0[:, 0:lo], T.x[:, 0:lo], "dx", [], [])
+    dma("s", T.xt0[:, hi:hi + lo], T.x[:, 0:lo], "dx", [], ["xt"])
     for r in range(16):
-        dma("s", T.pb[r:128:16, :], T.p[:], "dpb", [], [])
+        dma("a", T.pb[r:128:16, :], T.p[:], "dpb", [], [])
     wrote["pb"] = ("dpb", count["dpb"])
+    dma("s", T.pin[:], T.p[:], "dp", [], ["pin"])
     dma("s", T.wq[:].bitcast(dt.uint8), T.wc[:], "dw", [], [])
     dma("s", T.wp[:], T.ws[:], "dw", [], ["w"])
     dma("s", T.vt[:], T.v[:], "dv", [], ["vt"])
 
-    def iota(out, pattern, mul, key):
-        op("gc_", lambda: g.iota(out, pattern, 0, mul, allow_small_or_imprecise_dtypes=True), [], [key])
+    def iota(out, pattern, base, mul, key):
+        op("gc_", lambda: g.iota(out, pattern, base, mul, allow_small_or_imprecise_dtypes=True), [], [key])
 
     op("v", lambda: V.memset(T.eo[:], 1.0), [], ["eo"])
-    for name, k in (("nb", 0), ("nb", C + 16), ("gb", 0), ("gb", C + 16), ("wb", C - 16), ("wb", 2 * C)):
+    for name, k in (("gb", 0), ("gb", C + 16), ("wb", C - 16), ("wb", 2 * C)):
         op("v", lambda: V.memset(T[name][:, k:k + 16], 0.0), [], [name + "_pad"])
     wrote["wb"] = wrote["wb_pad"]
-    iota(T.c8[:], [[16, 8]], 0, "c8")
-    iota(T.pi[:], [[1, 1]], 1, "pi")
-    iota(T.ci[:], [[1, NC]], 0, "ci")
-    iota(T.j16[:], [[0, NC], [1, 16]], 0, "j16")
+    iota(T.c8[:], [[16, 8]], 0, 0, "c8")
+    iota(T.pi[:], [[1, 1]], 0, 1, "pi")
+    iota(T.ci[:], [[1, NC]], 0, 0, "ci")
+    iota(T.j16[:], [[0, NC], [1, 16]], 0, 0, "j16")
     op("gc_", lambda: g.affine_select(T.ee[:], T.eo[:], [[1, 516]], A.is_equal, 0.0, -3, -4), ["eo"], ["ee"])
-    iota(T.iof[:], [[1, C]], 0, "iof")
+    iota(T.iof[:], [[1, C]], 0, 0, "iof")
     cp(T.ul[:], T.c8[:], ["c8"], ["ul"])
     ts(T.qi[:], T.pi[:], 15, None, [A.bitwise_and], ["pi"], ["qi"])
-    ts(T.oi[:], T.pi[:], 16, None, [A.bitwise_and], ["pi"], ["oi"])
-    cp(T.qf[:], T.qi[:], ["qi"], ["qf"])
-    ts(T.me[:], T.oi[:], 0.0, None, [A.is_equal], ["oi"], ["me"])
-    ts(T.mo[:], T.oi[:], 0.0, None, [A.is_gt], ["oi"], ["mo"])
-    ts(T.q20[:], T.qf[:], 20.0, None, [A.mult], ["qf"], ["q20"])
+    ts(T.oi[:], T.pi[:], 16, 4, [A.bitwise_and, A.arith_shift_right], ["pi"], ["oi"])
     cp(T.exl[:], T.ci[:], ["ci"], ["exl"])
+    cp(T.qf[:], T.qi[:], ["qi"], ["qf"])
+    tt(T.si[:], T.qi[:], T.oi[:], A.add, ["qi", "oi"], ["si"])
+    ts(T.k2[:], T.qi[:], 16.0, None, [A.mult], ["qi"], ["k2"])
+    ts(T.q20[:], T.qf[:], 20.0, None, [A.mult], ["qf"], ["q20"])
+    ts(T.ri[:], T.si[:], 1, None, [A.bitwise_and], ["si"], ["ri"])
     ts(T.iw[:], T.ci[:], 16.0, T.qf[:, 0:1], [A.mult, A.add], ["ci", "qf"], ["iw"])
-    cp(T.ka[:, 0:NC], T.iw[:], ["iw"], ["kaw"])
+    ts(T.k1[:], T.ri[:], float(C + 16), None, [A.mult], ["ri"], ["k1"])
     ts(T.pbf[:], T.ci[:], T.q20[:, 0:1], None, [A.add], ["ci", "q20"], ["pbf"])
+    tt(T.k3[:], T.k1[:], T.k2[:], A.add, ["k1", "k2"], ["k3"])
+    cp(T.ka[:, 0:NC], T.iw[:], ["iw"], ["kaw"])
     cp(T.pbl[:], T.pbf[:], ["pbf"], ["pbl"])
+    cp(T.wl[:, 0:1], T.k3[:], ["k3"], ["wl0"])
+    ts(T.wl[:, 1:2], T.k3[:], 256.0, float(C + E - 1), [A.add, A.min], ["k3"], ["wl1"])
     ts(T.kk[:], T.j16[:], T.qf[:, 0:1], None, [A.is_gt], ["j16", "qf"], ["kk"])
 
     quant(T.uq[:], T.us[:], T.ut[:], ["ut"], ["uq"])
@@ -178,71 +194,72 @@ def rank_program(g, core, T, topo):
     for b in range(4):
         quant(T.eq[:, 128 * b:128 * b + 128], T.es[:, 128 * b:128 * b + 128], T.ee[:, 3 - b:515 - b], ["ee"], ["eq%d" % b])
 
-    def to_wrapped(buf, a, out, bkeys, okey, bank=None, bank_key=None):
-        if bank is None:
-            op("v", lambda: V.transpose(T.tt[:, 0:C], buf[:, a:a + C]), bkeys, ["tta"])
-        else:
-            op("v", lambda: V.transpose(T.tt[:, 0:C], bank[:, 0:C]), [bank_key], ["tta"])
-        op("v", lambda: V.transpose(T.tt[:, C:2 * C + 32], buf[:, a - 16:a + C + 16]), bkeys, ["ttb"])
-        e = 2 * C + 32
-        ts(T.w1[:, 0:21], T.tt[:, 0:e:32], T.me[:, 0:1], None, [A.mult], ["tta", "ttb", "me"], ["w1"])
-        ts(T.w2[:, 0:21], T.tt[:, 16:e:32], T.mo[:, 0:1], None, [A.mult], ["tta", "ttb", "mo"], ["w2"])
-        tt(out[:, 0:NC:2], T.w1[:, 0:10], T.w2[:, 10:20], A.add, ["w1", "w2"], [okey + "_even"])
-        tt(out[:, 1:NC:2], T.w1[:, 11:21], T.w2[:, 0:10], A.add, ["w1", "w2"], [okey + "_odd"])
+    def to_wrapped(buf, a, out, keys, okey):
+        op("v", lambda: V.transpose(T.tt[:, 0:C], buf[:, a:a + C]), keys, ["tta"])
+        op("v", lambda: V.transpose(T.tt[:, C:C + E], buf[:, a - 16:a + C + 16]), keys, ["ttb"])
+        cp(out[:], T.tt[:].indirect(T.wl[:]), ["tta", "ttb", "wl0", "wl1"], [okey])
 
     for t in range(ROUNDS):
         xt = T.xt0 if t == 0 else T.xt1
-        xk = ["xt"] if t == 0 else ["x%d" % b for b in range(4)]
+        xk = ["xt"] if t == 0 else ["x%d" % b for b in range(4)] + ["xpad"]
         qx, sx, qk = T["qx%d" % t], T["sx%d" % t], "qx%d" % t
         quant(qx[:], sx[:], xt[:], xk, [qk])
-        mm(T.ps5[:, 0:C], T.uqr[:], T.usr[:], qx[:], sx[:], ["uqr", "usr", qk], ["ps5"])
-        mm(T.ps0[:, 0:C], T.uqr[:], T.usr[:], qx[:], sx[:], ["uqr", "usr", qk], ["ps0"])
-        send(T["qp%d" % t][:].bitcast(dt.uint8), qx[:].bitcast(dt.uint8), "rq%d" % t, "lq%d" % t, [qk])
-        send(T["sp%d" % t][:], sx[:], "rq%d" % t, "lq%d" % t, [qk])
-        act(T.nb[:, 16:16 + C], T.ps5[:, 0:C], ["ps5"], ["nb"])
-        to_wrapped(T.nb, 16, T.sw, ["nb", "nb_pad"], "sw", T.ps0, "ps0")
-        sk = ["sw_even", "sw_odd"]
+        mm(T.ps0[:, 0:E], T.uqr[:], T.usr[:], qx[:], sx[:], ["uqr", "usr", qk], ["ps0"])
+        mm(T.ps5[:, 0:C], T.uqr[:], T.usr[:], qx[:, 16:16 + C], sx[:, 16:16 + C], ["uqr", "usr", qk], ["ps5"])
+        send(T["qp%d" % t][:].bitcast(dt.uint8), qx[:, 16:16 + C].bitcast(dt.uint8), "rq%d" % t, "lq%d" % t, [qk])
+        send(T["sp%d" % t][:], sx[:, 16:16 + C], "rq%d" % t, "lq%d" % t, [qk])
+        act(T.nb[:], T.ps5[:, 0:C], ["ps5"], ["nb"])
+        if t == 0:
+            iota(T.iog[:], [[1, C]], C, 0, "iog")
+            ts(T.l50[:], T.pb[:].indirect(T.pbl[:]), 512.0, None, [A.mult], ["pb", "pbl"], ["l50"])
+        to_wrapped(T.ps0, 16, T.sw, ["ps0"], "sw")
         for c in range(NC):
             f, e, sc = C * c, 16 * c + 16, T.sw[:, c:c + 1]
             fk = ["fl%d" % c, "fh%d" % c]
-            ts(T.fb[:, f:f + e], T.nb[:, 16:16 + e], sc, None, [A.is_ge], ["nb"] + sk, fk[:1])
+            ts(T.fb[:, f:f + e], T.nb[:, 0:e], sc, None, [A.is_ge], ["nb", "sw"], fk[:1])
             if e < C:
-                ts(T.fb[:, f + e:f + C], T.nb[:, 16 + e:16 + C], sc, None, [A.is_gt], ["nb"] + sk, fk[1:])
-            act(T.fb[:, f:f + C], T.fb[:, f:f + C], fk, fk + ["acc"], accum=T.acc[:, c:c + 1])
-            if c == 6:
-                act(T.ex[:], T.sw[:, 0:NC].indirect(T.exl[:]), sk + ["exl"], ["ex"])
+                ts(T.fb[:, f + e:f + C], T.nb[:, e:C], sc, None, [A.is_gt], ["nb", "sw"], fk[1:])
+            if c in ON_VECTOR:
+                op("v", lambda: V.tensor_reduce(T.acc[:, c:c + 1], T.fb[:, f:f + C], AxisListType.X, A.add), fk, ["acc%d" % c])
+            else:
+                act(T.fb[:, f:f + C], T.fb[:, f:f + C], fk, fk + ["acc%d" % c], accum=T.acc[:, c:c + 1])
+            if c == 4:
+                act(T.ex[:], T.sw[:].indirect(T.exl[:]), ["sw", "exl"], ["ex"])
             if c == 8 and t == 0:
-                ts(T.l50[:], T.pb[:].indirect(T.pbl[:]), 512.0, None, [A.mult], ["pb", "pbl"], ["l50"])
                 cp(T.lw0[:], T.pin[:], ["pin"], ["lw0"])
-                ts(T.iog[:], T.iof[:], float(C), None, [A.add], ["iof"], ["iog"])
                 tt(T.vb[:], T.l50[:], T.iof[:], A.add, ["l50", "iof"], ["vb"])
-        lw, ln, lk = T["lw%d" % t], T["lw%d" % (t + 1)], "lw%d" % t
-        ts(T.ka[:, NC:2 * NC], lw[:], float(1 - C), None, [A.add], [lk], ["kal"])
-        tt(T.te[:], T.ps0[:, 0:C], T.ex[:], A.is_equal, ["ps0", "ex"], ["te"])
-        op("v", lambda: V.tensor_tensor_scan(T.ts[:], T.te[:], T.kk[:], 0.0, A.add, A.mult), ["te", "kk"], ["ts"])
+            if c == 16:
+                tt(T.te[:], T.ps0[:, 16:16 + C], T.ex[:], A.is_equal, ["ps0", "ex"], ["te"])
+            if c == 17:
+                op("v", lambda: V.tensor_tensor_scan(T.ts[:], T.te[:], T.kk[:], 0.0, A.add, A.mult), ["te", "kk"], ["ts"])
+            if c == 18:
+                lw, ln, lk = T["lw%d" % t], T["lw%d" % (t + 1)], "lw%d" % t
+                ts(T.ka[:, NC:2 * NC], lw[:], float(1 - C), None, [A.add], [lk], ["kal"])
         for dst, w, key in ((T.hw, 2 * C, "h"), (T.hx, C, "g")):
             for b in range(4):
                 if t == 0:
-                    act(dst[:, w * b:w * b + C], T.xt0[:, b:4 * C:4], ["xt"], [key + str(b)], scale=0.5)
+                    act(dst[:, w * b:w * b + C], T.xt0[:, lo + b:hi:4], ["xt"], [key + str(b)], scale=0.5)
                 else:
                     act(dst[:, w * b:w * b + C], T.uu[:, C * b:C * b + C], ["uu%d" % b], [key + str(b)], scale=2.0 ** -6)
         for b in range(4):
             k = "ps%d" % (1 + b)
             mm(T[k][:, 0:C], T.eq[:, 128 * b:128 * b + 128], T.es[:, 128 * b:128 * b + 128], T["qp%d" % t][:], T["sp%d" % t][:], ["eq%d" % b, "qp%d" % t], [k])
             act(T.hw[:, 2 * C * b + C:2 * C * b + 2 * C], T[k][:, 0:C], [k], ["d%d" % b], scale=0.5)
-        tt(T.pli[:], T.acc[:], T.ts[:, 15:C:16], A.subtract, ["acc", "ts"], ["pli"])
-        ts(T.plu[:], T.pli[:], -1.0, None, [A.add], ["pli"], ["plu"])
+        if t == 0:
+            for k in (0, hi):
+                act(T.xt1[:, k:k + lo], T.xt0[:, k:k + lo], ["xt"], ["xpad"])
+        tt(T.pli[:], T.acc[:], T.ts[:, 15:C:16], A.subtract, ["acc%d" % c for c in range(NC)] + ["ts"], ["pli"])
         ts(T.par[:], T.pli[:], 1, None, [A.bitwise_and], ["pli"], ["par"])
-        op("v", lambda: V.tensor_copy(T.wo[:, 0:C].indirect(T.plu[:]), T.vb[:]), ["plu", "vb"], ["wo"])
+        ts(T.plu[:], T.pli[:], -1.0, None, [A.add], ["pli"], ["plu"])
         ts(T.alt[:], T.par[:], 2.0, -2.0, [A.mult, A.add], ["par"], ["alt"])
+        cp(T.wo[:].indirect(T.plu[:]), T.vb[:], ["plu", "vb"], ["wo"])
         tt(T.pxi[:], T.pli[:], T.alt[:], A.add, ["pli", "alt"], ["pxi"])
         cp(T.pxu[:], T.pxi[:], ["pxi"], ["pxu"])
-        cp(T.gb[:, 16:16 + C], T.wo[:, 0:C].indirect(T.pxu[:]), ["wo", "pxu"], ["gb"])
+        cp(T.gb[:, 16:16 + C], T.wo[:].indirect(T.pxu[:]), ["wo", "pxu"], ["gb"])
         to_wrapped(T.gb, 16, T.pv, ["gb", "gb_pad"], "pv")
-        pk = ["pv_even", "pv_odd"]
         lb, bi = T.bl[:, 0:NC], T.bl[:, NC:2 * NC]
-        ts(lb, T.pv[:], 9, None, [A.arith_shift_right], pk, ["lb"])
-        ts(bi, T.pv[:], 511, None, [A.bitwise_and], pk, ["bi"])
+        ts(lb, T.pv[:, 0:NC], 9, None, [A.arith_shift_right], ["pv"], ["lb"])
+        ts(bi, T.pv[:, 0:NC], 511, None, [A.bitwise_and], ["pv"], ["bi"])
         tt(T.xx[:], T.bl[:], T.ka[:], A.subtract, ["lb", "bi", "kaw", "kal"], ["xx"])
         tt(T.dl[:], lb, lw[:], A.subtract, ["lb", lk], ["dl"])
         ts(T.cl[:], T.xx[:], 0.0, float(C - 1), [A.max, A.min], ["xx"], ["cl"])
@@ -253,8 +270,8 @@ def rank_program(g, core, T, topo):
         lu, uk = T["lu%d" % t], "lu%d" % t
         cp(lu[:], ln[:], ["lw%d" % (t + 1)], [uk])
         send(T["la%d" % t][:], lu[:], "rl%d" % t, "ll%d" % t, [uk])
-        cp(T.wb[:, C:3 * C].indirect(lu[:]), T.iof[:], [uk, "iof"], ["wb"])
         tt(T.db[:], bi, T.iw[:], A.subtract, ["bi", "iw"], ["db"])
+        cp(T.wb[:, C:3 * C].indirect(lu[:]), T.iof[:], [uk, "iof"], ["wb"])
         tt(T.pm[:], T.mm[:], T.db[:], A.mult, ["mm", "db"], ["pm"])
         tt(T.pf[:], T.pm[:], T.iw[:], A.add, ["pm", "iw"], ["pf"])
         cp(T.pu[:], T.pf[:], ["pf"], ["pu"])
@@ -267,11 +284,10 @@ def rank_program(g, core, T, topo):
             dma("s", T.ol[:], T.olb[0:128:16, :], "dol", ["olb"], [])
             quant(T.vq[:], T.vs[:], T.vt[:], ["vt"], ["vq"])
         cp(T.wb[:, 0:2 * C].indirect(T["la%d" % t][:]), T.iog[:], ["la%d" % t, "iog"], ["wb"])
-        to_wrapped(T.wb, C, T.ef, ["wb"], "ef")
-        cp(T.eu[:], T.ef[:], ["ef_even", "ef_odd"], ["eu"])
+        to_wrapped(T.wb, C, T.eu, ["wb"], "eu")
         for b in range(4):
             o = 2 * C * b
-            tt(T.z[:, b:4 * C:4], T.hw[:, o:o + 2 * C].indirect(T.eu[:]), T.hx[:, C * b:C * b + C], A.add, ["eu", "h%d" % b, "g%d" % b, "d%d" % b], ["z%d" % b])
+            tt(T.z[:, b:4 * C:4], T.hw[:, o:o + 2 * C].indirect(T.eu[:, 0:NC]), T.hx[:, C * b:C * b + C], A.add, ["eu", "h%d" % b, "g%d" % b, "d%d" % b], ["z%d" % b])
             act(T.z32[:, C * b:C * b + C], T.z[:, b:4 * C:4], ["z%d" % b], ["zz%d" % b], scale=32.0)
         quant(T.zq[:], T.zs[:], T.z[:], ["z%d" % b for b in range(4)], ["zq"])
         for b in range(4):
@@ -280,12 +296,12 @@ def rank_program(g, core, T, topo):
             mm(T[k][:, 0:C], T.wq[:, 128 * b:128 * b + 128], T.wp[:, 128 * b:128 * b + 128], T.zq[:], T.zs[:], ["w", "zq"], [k])
             tt(u, T[k][:, 0:C], T.z32[:, C * b:C * b + C], A.add, [k, "zz%d" % b], ["uu%d" % b])
             if b < 3:
-                act(T.xt1[:, b:4 * C:4], u, ["uu%d" % b], ["x%d" % b], scale=2.0 ** -5)
+                act(T.xt1[:, lo + b:hi:4], u, ["uu%d" % b], ["x%d" % b], scale=2.0 ** -5)
             else:
-                ts(T.xt1[:, b:4 * C:4], u, 2.0 ** -5, None, [A.mult], ["uu%d" % b], ["x%d" % b])
+                ts(T.xt1[:, lo + b:hi:4], u, 2.0 ** -5, None, [A.mult], ["uu%d" % b], ["x%d" % b])
 
     q3, s3 = T["qx%d" % ROUNDS], T["sx%d" % ROUNDS]
-    quant(q3[:], s3[:], T.xt1[:], ["x%d" % b for b in range(4)], ["q3"])
+    quant(q3[:], s3[:], T.xt1[:, lo:hi], ["x%d" % b for b in range(4)], ["q3"])
     mm(T.ps0[:, 0:C], T.vq[:], T.vs[:], q3[:], s3[:], ["vq", "q3"], ["ps0"])
     dma("s", T.oc[:], q3[:].bitcast(dt.uint8), "doc", ["q3"], [])
     for k in range(4):

@@ -4,8 +4,8 @@ A = AluOpType
 COPY = ActivationFunctionType.Copy
 C, ROUNDS = 320, 3
 E = C + 32
+M = C // 2
 NC = C // 16
-ON_VECTOR = (NC - 1,)
 F8 = "float8_e4m3fn_x4"
 
 SCRATCH = {}
@@ -34,14 +34,12 @@ _declare("sx0 sx1 sx2", E, "uint8")
 _declare("gb", E, "float32")
 _declare("wb", 3 * C, "float32")
 _declare("tt", C + E, "float32")
-_declare("nb ex vb wo j16 iof iog yb olb l50 l51 l52", C, "float32")
-_declare("sw", 32, "float32")
-_declare("acc alt pxi dl mm md db pm pf ci iw pbf lw0 lw1 lw2 lw3", NC, "float32")
-_declare("xx cl ok ka", 2 * NC, "float32")
+_declare("nb ex vb wo j16 iof iog iov yb olb l50 l51 l52", C, "float32")
+_declare("sw qa qb ka kb", 32, "float32")
+_declare("acc pq pxi xb ca cb oa ob dl ls m1 md mm e5 f1 db pm pf ci iw pbf lw0 lw1 lw2 lw3", NC, "float32")
 _declare("qf q20 k1 k2 k3", 1, "float32")
-_declare("pli par pin", NC, "int32")
-_declare("pv", 32, "int32")
-_declare("bl", 2 * NC, "int32")
+_declare("pli hh pin", NC, "int32")
+_declare("bl", 32, "int32")
 _declare("pb", C, "int32")
 _declare("c8", 8, "int32")
 _declare("pi qi oi si ri", 1, "int32")
@@ -160,9 +158,9 @@ def rank_program(g, core, T, topo):
         op("gc_", lambda: g.iota(out, pattern, base, mul, allow_small_or_imprecise_dtypes=True), [], [key])
 
     op("v", lambda: V.memset(T.eo[:], 1.0), [], ["eo"])
-    for name, k in (("gb", 0), ("gb", C + 16), ("wb", C - 16), ("wb", 2 * C)):
-        op("v", lambda: V.memset(T[name][:, k:k + 16], 0.0), [], [name + "_pad"])
-    wrote["wb"] = wrote["wb_pad"]
+    for name, k, w in (("gb", 0, 16), ("gb", C + 16, 16), ("wb", C - 16, 16), ("wb", 2 * C, 16), ("ka", 20, 12), ("kb", 20, 12)):
+        op("v", lambda: V.memset(T[name][:, k:k + w], 0.0), [], ["%s_pad%d" % (name, k)])
+    wrote["gb_pad"], wrote["wb"] = wrote["gb_pad%d" % (C + 16)], wrote["wb_pad%d" % (2 * C)]
     iota(T.c8[:], [[16, 8]], 0, 0, "c8")
     iota(T.pi[:], [[1, 1]], 0, 1, "pi")
     iota(T.ci[:], [[1, NC]], 0, 0, "ci")
@@ -182,7 +180,7 @@ def rank_program(g, core, T, topo):
     ts(T.k1[:], T.ri[:], float(C + 16), None, [A.mult], ["ri"], ["k1"])
     ts(T.pbf[:], T.ci[:], T.q20[:, 0:1], None, [A.add], ["ci", "q20"], ["pbf"])
     tt(T.k3[:], T.k1[:], T.k2[:], A.add, ["k1", "k2"], ["k3"])
-    cp(T.ka[:, 0:NC], T.iw[:], ["iw"], ["kaw"])
+    cp(T.ka[:, 0:NC], T.iw[:], ["iw"], ["ka"])
     cp(T.pbl[:], T.pbf[:], ["pbf"], ["pbl"])
     cp(T.wl[:, 0:1], T.k3[:], ["k3"], ["wl0"])
     ts(T.wl[:, 1:2], T.k3[:], 256.0, float(C + E - 1), [A.add, A.min], ["k3"], ["wl1"])
@@ -194,32 +192,50 @@ def rank_program(g, core, T, topo):
     for b in range(4):
         quant(T.eq[:, 128 * b:128 * b + 128], T.es[:, 128 * b:128 * b + 128], T.ee[:, 3 - b:515 - b], ["ee"], ["eq%d" % b])
 
-    def to_wrapped(buf, a, out, keys, okey):
-        op("v", lambda: V.transpose(T.tt[:, 0:C], buf[:, a:a + C]), keys, ["tta"])
-        op("v", lambda: V.transpose(T.tt[:, C:C + E], buf[:, a - 16:a + C + 16]), keys, ["ttb"])
-        cp(out[:], T.tt[:].indirect(T.wl[:]), ["tta", "ttb", "wl0", "wl1"], [okey])
+    def turn(at, in_, keys, key):
+        w = in_.shape[1]
+        op("v", lambda: V.transpose(T.tt[:, at:at + w], in_), keys, [key])
+
+    turned = T.tt[:].indirect(T.wl[:])
+    wlk = ["wl0", "wl1"]
 
     for t in range(ROUNDS):
         xt = T.xt0 if t == 0 else T.xt1
-        xk = ["xt"] if t == 0 else ["x%d" % b for b in range(4)] + ["xpad"]
-        qx, sx, qk = T["qx%d" % t], T["sx%d" % t], "qx%d" % t
-        quant(qx[:], sx[:], xt[:], xk, [qk])
-        mm(T.ps0[:, 0:E], T.uqr[:], T.usr[:], qx[:], sx[:], ["uqr", "usr", qk], ["ps0"])
-        mm(T.ps5[:, 0:C], T.uqr[:], T.usr[:], qx[:, 16:16 + C], sx[:, 16:16 + C], ["uqr", "usr", qk], ["ps5"])
-        send(T["qp%d" % t][:].bitcast(dt.uint8), qx[:, 16:16 + C].bitcast(dt.uint8), "rq%d" % t, "lq%d" % t, [qk])
-        send(T["sp%d" % t][:], sx[:, 16:16 + C], "rq%d" % t, "lq%d" % t, [qk])
-        act(T.nb[:], T.ps5[:, 0:C], ["ps5"], ["nb"])
+        qx, sx, qk = T["qx%d" % t], T["sx%d" % t], ["qx%d_0" % t, "qx%d_1" % t]
+        if t == 0:
+            quant(qx[:, 0:16 + M], sx[:, 0:16 + M], xt[:, 0:lo + 4 * M], ["xt"], qk[:1])
+            quant(qx[:, 16 + M:E], sx[:, 16 + M:E], xt[:, lo + 4 * M:4 * E], ["xt"], qk[1:])
+        else:
+            quant(qx[:, 0:16 + M], sx[:, 0:16 + M], xt[:, 0:lo + 4 * M], ["x%d_0" % b for b in range(4)] + ["xpad0"], qk[:1])
+            ts(xt[:, lo + 4 * M + 3:hi:4], T.uu[:, 3 * C + M:4 * C], 2.0 ** -5, None, [A.mult], ["uu3_1"], ["x3_1"])
+            quant(qx[:, 16 + M:E], sx[:, 16 + M:E], xt[:, lo + 4 * M:4 * E], ["x%d_1" % b for b in range(4)] + ["xpad1"], qk[1:])
+        uk = ["uqr", "usr"]
+        mm(T.ps6[:, 0:16 + M], T.uqr[:], T.usr[:], qx[:, 0:16 + M], sx[:, 0:16 + M], uk + qk[:1], ["ps6"])
+        mm(T.ps0[:, 0:M], T.uqr[:], T.usr[:], qx[:, 16:16 + M], sx[:, 16:16 + M], uk + qk[:1], ["ps0"])
+        mm(T.ps7[:, 0:32 + M], T.uqr[:], T.usr[:], qx[:, M:E], sx[:, M:E], uk + qk, ["ps7"])
+        mm(T.ps5[:, 0:M], T.uqr[:], T.usr[:], qx[:, 16 + M:16 + C], sx[:, 16 + M:16 + C], uk + qk[1:], ["ps5"])
+        send(T["qp%d" % t][:].bitcast(dt.uint8), qx[:, 16:16 + C].bitcast(dt.uint8), "rq%d" % t, "lq%d" % t, qk)
+        send(T["sp%d" % t][:], sx[:, 16:16 + C], "rq%d" % t, "lq%d" % t, qk)
+        act(T.nb[:, 0:M], T.ps0[:, 0:M], ["ps0"], ["nb0"])
+        act(T.nb[:, M:C], T.ps5[:, 0:M], ["ps5"], ["nb1"])
         if t == 0:
             iota(T.iog[:], [[1, C]], C, 0, "iog")
-            ts(T.l50[:], T.pb[:].indirect(T.pbl[:]), 512.0, None, [A.mult], ["pb", "pbl"], ["l50"])
-        to_wrapped(T.ps0, 16, T.sw, ["ps0"], "sw")
+            cp(T.l50[:], T.pb[:].indirect(T.pbl[:]), ["pb", "pbl"], ["l50"])
+        turn(0, T.ps6[:, 16:16 + M], ["ps6"], "ta0")
+        turn(C, T.ps6[:, 0:M], ["ps6"], "tb0")
+        turn(M, T.ps7[:, 16:16 + M], ["ps7"], "ta1")
+        turn(C + M, T.ps7[:, 0:32 + M], ["ps7"], "tb1")
+        tk = ["ta0", "tb0", "ta1", "tb1"]
+        cp(T.sw[:], turned, tk + wlk, ["sw"])
+        sk = ["nb0", "nb1", "sw"]
+        lw, ln, lk = T["lw%d" % t], T["lw%d" % (t + 1)], "lw%d" % t
         for c in range(NC):
             f, e, sc = C * c, 16 * c + 16, T.sw[:, c:c + 1]
             fk = ["fl%d" % c, "fh%d" % c]
-            ts(T.fb[:, f:f + e], T.nb[:, 0:e], sc, None, [A.is_ge], ["nb", "sw"], fk[:1])
+            ts(T.fb[:, f:f + e], T.nb[:, 0:e], sc, None, [A.is_ge], sk, fk[:1])
             if e < C:
-                ts(T.fb[:, f + e:f + C], T.nb[:, e:C], sc, None, [A.is_gt], ["nb", "sw"], fk[1:])
-            if c in ON_VECTOR:
+                ts(T.fb[:, f + e:f + C], T.nb[:, e:C], sc, None, [A.is_gt], sk, fk[1:])
+            if c == NC - 1:
                 op("v", lambda: V.tensor_reduce(T.acc[:, c:c + 1], T.fb[:, f:f + C], AxisListType.X, A.add), fk, ["acc%d" % c])
             else:
                 act(T.fb[:, f:f + C], T.fb[:, f:f + C], fk, fk + ["acc%d" % c], accum=T.acc[:, c:c + 1])
@@ -227,87 +243,112 @@ def rank_program(g, core, T, topo):
                 act(T.ex[:], T.sw[:].indirect(T.exl[:]), ["sw", "exl"], ["ex"])
             if c == 8 and t == 0:
                 cp(T.lw0[:], T.pin[:], ["pin"], ["lw0"])
-                tt(T.vb[:], T.l50[:], T.iof[:], A.add, ["l50", "iof"], ["vb"])
+                ts(T.iov[:], T.iof[:], float(-M), 2.0 ** -9, [A.add, A.mult], ["iof"], ["iov"])
+            if c == 10 and t == 0:
+                tt(T.vb[:], T.l50[:], T.iov[:], A.add, ["l50", "iov"], ["vb"])
+            if c == 15:
+                ts(T.kb[:, 0:NC], lw[:], float(-M), 2.0 ** -9, [A.add, A.mult], [lk], ["kb"])
+                tt(T.f1[:], lw[:], T.iw[:], A.subtract, [lk, "iw"], ["f1"])
             if c == 16:
-                tt(T.te[:], T.ps0[:, 16:16 + C], T.ex[:], A.is_equal, ["ps0", "ex"], ["te"])
+                tt(T.te[:, 0:M], T.ps0[:, 0:M], T.ex[:, 0:M], A.is_equal, ["ps0", "ex"], ["te0"])
+                tt(T.te[:, M:C], T.ps5[:, 0:M], T.ex[:, M:C], A.is_equal, ["ps5", "ex"], ["te1"])
             if c == 17:
-                op("v", lambda: V.tensor_tensor_scan(T.ts[:], T.te[:], T.kk[:], 0.0, A.add, A.mult), ["te", "kk"], ["ts"])
-            if c == 18:
-                lw, ln, lk = T["lw%d" % t], T["lw%d" % (t + 1)], "lw%d" % t
-                ts(T.ka[:, NC:2 * NC], lw[:], float(1 - C), None, [A.add], [lk], ["kal"])
+                op("v", lambda: V.tensor_tensor_scan(T.ts[:], T.te[:], T.kk[:], 0.0, A.add, A.mult), ["te0", "te1", "kk"], ["ts"])
         for dst, w, key in ((T.hw, 2 * C, "h"), (T.hx, C, "g")):
             for b in range(4):
                 if t == 0:
                     act(dst[:, w * b:w * b + C], T.xt0[:, lo + b:hi:4], ["xt"], [key + str(b)], scale=0.5)
                 else:
-                    act(dst[:, w * b:w * b + C], T.uu[:, C * b:C * b + C], ["uu%d" % b], [key + str(b)], scale=2.0 ** -6)
+                    act(dst[:, w * b:w * b + C], T.uu[:, C * b:C * b + C], ["uu%d_0" % b, "uu%d_1" % b], [key + str(b)], scale=2.0 ** -6)
         for b in range(4):
             k = "ps%d" % (1 + b)
             mm(T[k][:, 0:C], T.eq[:, 128 * b:128 * b + 128], T.es[:, 128 * b:128 * b + 128], T["qp%d" % t][:], T["sp%d" % t][:], ["eq%d" % b, "qp%d" % t], [k])
             act(T.hw[:, 2 * C * b + C:2 * C * b + 2 * C], T[k][:, 0:C], [k], ["d%d" % b], scale=0.5)
         if t == 0:
-            for k in (0, hi):
-                act(T.xt1[:, k:k + lo], T.xt0[:, k:k + lo], ["xt"], ["xpad"])
+            for i, k in enumerate((0, hi)):
+                act(T.xt1[:, k:k + lo], T.xt0[:, k:k + lo], ["xt"], ["xpad%d" % i])
         tt(T.pli[:], T.acc[:], T.ts[:, 15:C:16], A.subtract, ["acc%d" % c for c in range(NC)] + ["ts"], ["pli"])
-        ts(T.par[:], T.pli[:], 1, None, [A.bitwise_and], ["pli"], ["par"])
+        ts(T.hh[:], T.pli[:], -1.5, 0.5, [A.add, A.mult], ["pli"], ["hh"])
+        ts(T.pq[:], T.pli[:], 0.25, None, [A.mult], ["pli"], ["pq"])
         ts(T.plu[:], T.pli[:], -1.0, None, [A.add], ["pli"], ["plu"])
-        ts(T.alt[:], T.par[:], 2.0, -2.0, [A.mult, A.add], ["par"], ["alt"])
+        tt(T.pxi[:], T.hh[:], T.pq[:], A.subtract, ["hh", "pq"], ["pxi"])
         cp(T.wo[:].indirect(T.plu[:]), T.vb[:], ["plu", "vb"], ["wo"])
-        tt(T.pxi[:], T.pli[:], T.alt[:], A.add, ["pli", "alt"], ["pxi"])
-        cp(T.pxu[:], T.pxi[:], ["pxi"], ["pxu"])
+        ts(T.pxu[:], T.pxi[:], 4.0, 2.0, [A.mult, A.add], ["pxi"], ["pxu"])
         cp(T.gb[:, 16:16 + C], T.wo[:].indirect(T.pxu[:]), ["wo", "pxu"], ["gb"])
-        to_wrapped(T.gb, 16, T.pv, ["gb", "gb_pad"], "pv")
-        lb, bi = T.bl[:, 0:NC], T.bl[:, NC:2 * NC]
-        ts(lb, T.pv[:, 0:NC], 9, None, [A.arith_shift_right], ["pv"], ["lb"])
-        ts(bi, T.pv[:, 0:NC], 511, None, [A.bitwise_and], ["pv"], ["bi"])
-        tt(T.xx[:], T.bl[:], T.ka[:], A.subtract, ["lb", "bi", "kaw", "kal"], ["xx"])
-        tt(T.dl[:], lb, lw[:], A.subtract, ["lb", lk], ["dl"])
-        ts(T.cl[:], T.xx[:], 0.0, float(C - 1), [A.max, A.min], ["xx"], ["cl"])
-        tt(T.ok[:], T.cl[:], T.xx[:], A.is_equal, ["cl", "xx"], ["ok"])
-        tt(T.mm[:], T.ok[:, 0:NC], T.ok[:, NC:2 * NC], A.mult, ["ok"], ["mm"])
-        tt(T.md[:], T.mm[:], T.dl[:], A.mult, ["mm", "dl"], ["md"])
+        turn(0, T.gb[:, 16:16 + C], ["gb", "ta1"], "ta0")
+        turn(C, T.gb[:], ["gb", "gb_pad", "tb1"], "tb0")
+        cp(T.bl[:], turned, ["ta0", "tb0"] + wlk, ["bl"])
+        tt(T.qb[:], turned, T.kb[:], A.subtract, ["ta0", "tb0", "kb", "kb_pad20"] + wlk, ["qb"])
+        tt(T.qa[:], turned, T.ka[:], A.subtract, ["ta0", "tb0", "ka", "ka_pad20"] + wlk, ["qa"])
+        tt(T.xb[:], T.bl[:, 0:NC], T.qb[:, 0:NC], A.subtract, ["bl", "qb"], ["xb"])
+        ts(T.ca[:], T.qa[:, 0:NC], -0.4, C - 0.6, [A.max, A.min], ["qa"], ["ca"])
+        tt(T.dl[:], T.bl[:, 0:NC], lw[:], A.subtract, ["bl", lk], ["dl"])
+        ts(T.cb[:], T.xb[:], 0.0, (C - 1) / 512.0, [A.max, A.min], ["xb"], ["cb"])
+        tt(T.oa[:], T.ca[:], T.qa[:, 0:NC], A.is_equal, ["ca", "qa"], ["oa"])
+        ts(T.e5[:], T.xb[:], -512.0, None, [A.mult], ["xb"], ["e5"])
+        tt(T.ob[:], T.cb[:], T.xb[:], A.is_equal, ["cb", "xb"], ["ob"])
+        tt(T.m1[:], T.oa[:], T.dl[:], A.mult, ["oa", "dl"], ["m1"])
+        tt(T.db[:], T.f1[:], T.e5[:], A.add, ["f1", "e5"], ["db"])
+        tt(T.md[:], T.m1[:], T.ob[:], A.mult, ["m1", "ob"], ["md"])
+        tt(T.mm[:], T.oa[:], T.ob[:], A.mult, ["oa", "ob"], ["mm"])
         tt(ln[:], lw[:], T.md[:], A.add, [lk, "md"], ["lw%d" % (t + 1)])
-        lu, uk = T["lu%d" % t], "lu%d" % t
-        cp(lu[:], ln[:], ["lw%d" % (t + 1)], [uk])
-        send(T["la%d" % t][:], lu[:], "rl%d" % t, "ll%d" % t, [uk])
-        tt(T.db[:], bi, T.iw[:], A.subtract, ["bi", "iw"], ["db"])
-        cp(T.wb[:, C:3 * C].indirect(lu[:]), T.iof[:], [uk, "iof"], ["wb"])
         tt(T.pm[:], T.mm[:], T.db[:], A.mult, ["mm", "db"], ["pm"])
+        lu, luk = T["lu%d" % t], "lu%d" % t
+        cp(lu[:], ln[:], ["lw%d" % (t + 1)], [luk])
+        send(T["la%d" % t][:], lu[:], "rl%d" % t, "ll%d" % t, [luk])
         tt(T.pf[:], T.pm[:], T.iw[:], A.add, ["pm", "iw"], ["pf"])
+        cp(T.wb[:, C:3 * C].indirect(lu[:]), T.iof[:], [luk, "iof"], ["wb"])
         cp(T.pu[:], T.pf[:], ["pf"], ["pu"])
         l5, l5k = T["l5%d" % t], "l5%d" % t
         if t + 1 < ROUNDS:
             act(T["l5%d" % (t + 1)][:], l5[:].indirect(T.pu[:]), [l5k, "pu"], ["l5%d" % (t + 1)])
-            tt(T.vb[:], l5[:].indirect(T.pu[:]), T.iof[:], A.add, [l5k, "pu", "iof"], ["vb"])
+            tt(T.vb[:], l5[:].indirect(T.pu[:]), T.iov[:], A.add, [l5k, "pu", "iov"], ["vb"])
         else:
-            act(T.olb[:], l5[:].indirect(T.pu[:]), [l5k, "pu"], ["olb"], scale=2.0 ** -9)
+            act(T.olb[:], l5[:].indirect(T.pu[:]), [l5k, "pu"], ["olb"])
             dma("s", T.ol[:], T.olb[0:128:16, :], "dol", ["olb"], [])
             quant(T.vq[:], T.vs[:], T.vt[:], ["vt"], ["vq"])
         cp(T.wb[:, 0:2 * C].indirect(T["la%d" % t][:]), T.iog[:], ["la%d" % t, "iog"], ["wb"])
-        to_wrapped(T.wb, C, T.eu, ["wb"], "eu")
-        for b in range(4):
-            o = 2 * C * b
-            tt(T.z[:, b:4 * C:4], T.hw[:, o:o + 2 * C].indirect(T.eu[:, 0:NC]), T.hx[:, C * b:C * b + C], A.add, ["eu", "h%d" % b, "g%d" % b, "d%d" % b], ["z%d" % b])
-            act(T.z32[:, C * b:C * b + C], T.z[:, b:4 * C:4], ["z%d" % b], ["zz%d" % b], scale=32.0)
-        quant(T.zq[:], T.zs[:], T.z[:], ["z%d" % b for b in range(4)], ["zq"])
-        for b in range(4):
-            k = ("ps5", "ps6", "ps7", "ps1")[b]
-            u = T.uu[:, C * b:C * b + C]
-            mm(T[k][:, 0:C], T.wq[:, 128 * b:128 * b + 128], T.wp[:, 128 * b:128 * b + 128], T.zq[:], T.zs[:], ["w", "zq"], [k])
-            tt(u, T[k][:, 0:C], T.z32[:, C * b:C * b + C], A.add, [k, "zz%d" % b], ["uu%d" % b])
-            if b < 3:
-                act(T.xt1[:, lo + b:hi:4], u, ["uu%d" % b], ["x%d" % b], scale=2.0 ** -5)
-            else:
-                ts(T.xt1[:, lo + b:hi:4], u, 2.0 ** -5, None, [A.mult], ["uu%d" % b], ["x%d" % b])
+        turn(0, T.wb[:, C:2 * C], ["wb"], "ta0")
+        turn(C, T.wb[:, C - 16:2 * C + 16], ["wb"], "tb0")
+        cp(T.eu[:], turned, ["ta0", "tb0"] + wlk, ["eu"])
+        for b, h, n in ((0, 0, 2), (1, 0, 2), (2, 0, 2), (3, 0, 1), (3, 1, 1)):
+            o, j, w = 2 * C * b, M * h, M * n
+            zk = ["z%d_%d" % (b, i) for i in range(h, h + n)]
+            tt(T.z[:, 4 * j + b:4 * (j + w):4], T.hw[:, o:o + 2 * C].indirect(T.eu[:, j // 16:(j + w) // 16]), T.hx[:, C * b + j:C * b + j + w], A.add,
+               ["eu", "h%d" % b, "g%d" % b, "d%d" % b], zk)
+            act(T.z32[:, C * b + j:C * b + j + w], T.z[:, 4 * j + b:4 * (j + w):4], zk, ["zz%d_%d" % (b, i) for i in range(h, h + n)], scale=32.0)
+        banks = (("ps6", "ps7", "ps1", "ps2"), ("ps3", "ps4", "ps0", "ps5"))
+        for h in range(2):
+            j = M * h
+            quant(T.zq[:, j:j + M], T.zs[:, j:j + M], T.z[:, 4 * j:4 * (j + M)], ["z%d_%d" % (b, h) for b in range(4)], ["zq%d" % h])
+            for b in range(4):
+                k = banks[h][b]
+                mm(T[k][:, 0:M], T.wq[:, 128 * b:128 * b + 128], T.wp[:, 128 * b:128 * b + 128], T.zq[:, j:j + M], T.zs[:, j:j + M], ["w", "zq%d" % h], [k])
+        for h in range(2):
+            j = M * h
+            for b in range(4):
+                k, u = banks[h][b], T.uu[:, C * b + j:C * b + j + M]
+                tt(u, T[k][:, 0:M], T.z32[:, C * b + j:C * b + j + M], A.add, [k, "zz%d_%d" % (b, h)], ["uu%d_%d" % (b, h)])
+                if b < 3:
+                    act(T.xt1[:, lo + 4 * j + b:lo + 4 * (j + M):4], u, ["uu%d_%d" % (b, h)], ["x%d_%d" % (b, h)], scale=2.0 ** -5)
+                if (b, h) == (0, 1):
+                    ts(T.xt1[:, lo + 3:lo + 4 * M:4], T.uu[:, 3 * C:3 * C + M], 2.0 ** -5, None, [A.mult], ["uu3_0"], ["x3_0"])
 
     q3, s3 = T["qx%d" % ROUNDS], T["sx%d" % ROUNDS]
-    quant(q3[:], s3[:], T.xt1[:, lo:hi], ["x%d" % b for b in range(4)], ["q3"])
-    mm(T.ps0[:, 0:C], T.vq[:], T.vs[:], q3[:], s3[:], ["vq", "q3"], ["ps0"])
-    dma("s", T.oc[:], q3[:].bitcast(dt.uint8), "doc", ["q3"], [])
+    for h in range(2):
+        j, k = M * h, ("ps6", "ps7")[h]
+        if h:
+            ts(T.xt1[:, lo + 4 * M + 3:hi:4], T.uu[:, 3 * C + M:4 * C], 2.0 ** -5, None, [A.mult], ["uu3_1"], ["x3_1"])
+        quant(q3[:, j:j + M], s3[:, j:j + M], T.xt1[:, lo + 4 * j:lo + 4 * (j + M)], ["x%d_%d" % (b, h) for b in range(4)], ["q3_%d" % h])
+        mm(T[k][:, 0:M], T.vq[:], T.vs[:], q3[:, j:j + M], s3[:, j:j + M], ["vq", "q3_%d" % h], [k])
+    for h in range(2):
+        j, k = M * h, ("ps6", "ps7")[h]
+        cp(T.yb[:, j:j + M], T[k][:, 0:M], [k], ["yb%d" % h])
+        dma("as"[h], T.y[:, j:j + M], T.yb[:, j:j + M], "dy", ["yb%d" % h], [])
+    qk = ["q3_0", "q3_1"]
+    dma("a", T.oc[:], q3[:].bitcast(dt.uint8), "doc", qk, [])
     for k in range(4):
-        dma("s", T.osc[4 * k:4 * k + 4, :], s3[32 * k:32 * k + 4, :], "doc", ["q3"], [])
-    act(T.yb[:], T.ps0[:, 0:C], ["ps0"], ["yb"])
-    dma("a", T.y[:], T.yb[:], "dy", ["yb"], [])
+        dma("s" if k % 2 else "a", T.osc[4 * k:4 * k + 4, :], s3[32 * k:32 * k + 4, :], "doc", qk, [])
     for t in range(ROUNDS):
         count["rq%d" % t], count["rl%d" % t] = 2 * nmask, nmask
     need("s", [(s, m) for s, m in count.items()])

from concourse.mybir import dt, AluOpType, ActivationFunctionType, AxisListType

A = AluOpType
COPY = ActivationFunctionType.Copy
C, ROUNDS = 320, 3
E = C + 32
M = C // 2
NC = C // 16
F8 = "float8_e4m3fn_x4"

SCRATCH = {}


def _declare(names, columns, dtype, where="sbuf"):
    for name in names.split():
        SCRATCH[name] = (where, [128, columns], dtype)


_declare("xt0 xt1", 4 * E, "bfloat16")
_declare("z z32 uu hx", 4 * C, "bfloat16")
_declare("ut vt", 512, "bfloat16")
_declare("eo ee", 516, "bfloat16")
_declare("hw", 8 * C, "bfloat16")
_declare("fb", NC * C, "bfloat16")
_declare("te ts kk", C, "bfloat16")
_declare("uq uqr vq", 128, F8)
_declare("us usr vs", 128, "uint8")
_declare("wq eq", 512, F8)
_declare("wp es", 512, "uint8")
_declare("zq qx3 qp0 qp1 qp2", C, F8)
_declare("zs sx3 sp0 sp1 sp2", C, "uint8")
_declare("qx0 qx1 qx2", E, F8)
_declare("sx0 sx1 sx2", E, "uint8")
_declare("gb", E, "float32")
_declare("wb", 3 * C, "float32")
_declare("tt", C + E, "float32")
_declare("nb ex vb wo j16 iof iog iov yb olb l50 l51 l52", C, "float32")
_declare("sw qa qb ka kb", 32, "float32")
_declare("acc pq pxi xb ca cb oa ob dl ls m1 md mm e5 f1 db pm pf ci iw pbf lw0 lw1 lw2 lw3", NC, "float32")
_declare("qf q20 k1 k2 k3", 1, "float32")
_declare("pli hh pin", NC, "int32")
_declare("bl", 32, "int32")
_declare("pb", C, "int32")
_declare("c8", 8, "int32")
_declare("pi qi oi si ri", 1, "int32")
_declare("plu pxu pu exl pbl lu0 lu1 lu2 la0 la1 la2", NC, "uint16")
_declare("eu", 32, "uint16")
_declare("ul", 8, "uint16")
_declare("wl", 2, "uint16")
_declare("ps0 ps1 ps2 ps3 ps4 ps5 ps6 ps7", 512, "float32", "psum")

SEMAPHORES = (["v", "a", "t", "gc_", "dx", "du", "dp", "dpb", "dw", "dv", "dy", "dol", "doc"]
              + ["%s%d" % (n, t) for n in ("rq", "rl", "lq", "ll") for t in range(ROUNDS)])


def rank_program(g, core, T, topo):
    rank = T.rank_of(core)
    if rank is None:
        return
    nxt = T.cores[(rank + 1) % len(T.cores)]
    rid, pid = topo.addr(nxt)[:2]
    mask = topo.mask(core, nxt)
    nmask = len(topo.engines(core, nxt))
    eng = {"v": g.vector, "a": g.scalar, "t": g.tensor, "gc_": g, "s": g.sync}

    count, known, snap = {}, {q: {} for q in eng}, {}
    wrote, read, order = {}, {}, [0]

    def need(q, toks):
        for k in sorted(set(toks), key=lambda k: (snap.get(k, (0, {}))[0], k), reverse=True):
            if known[q].get(k[0], 0) >= k[1]:
                continue
            eng[q].wait_ge(T.sem[k[0]], k[1])
            for s, m in list(snap.get(k, (0, {}))[1].items()) + [k]:
                if known[q].get(s, 0) < m:
                    known[q][s] = m

    def deps(q, reads, writes):
        toks = []
        for k in reads:
            if k in wrote:
                toks.append(wrote[k])
            if k[:2] == "ps":
                toks += [(s, m) for s, m in read.get(k, {}).items() if s != q]
        for k in writes:
            if k in wrote:
                toks.append(wrote[k])
            toks += [(s, m) for s, m in read.get(k, {}).items() if s != q]
        return toks

    def note(tok, reads, writes, q):
        order[0] += 1
        snap[tok] = (order[0], dict(known[q]))
        for k in reads:
            read.setdefault(k, {})[tok[0]] = tok[1]
        for k in writes:
            wrote[k] = tok
            read[k] = {}

    def op(q, fn, reads, writes):
        need(q, deps(q, reads, writes))
        fn().then_inc(T.sem[q], 1)
        count[q] = count.get(q, 0) + 1
        note((q, count[q]), reads, writes, q)

    def dma(q, out, in_, sem, reads, writes):
        need(q, deps(q, reads, writes))
        eng[q].dma_start(out, in_).then_inc(T.sem[sem], 16)
        count[sem] = count.get(sem, 0) + 16
        note((sem, count[sem]), reads, writes, q)

    def send(out, in_, rsem, lsem, reads):
        need("gc_", deps("gc_", reads, []))
        g.remote_dma(out, in_, T.sem[rsem], T.sem[lsem], pid, rid, mask)
        count[lsem] = count.get(lsem, 0) + nmask

    V, S, P = g.vector, g.scalar, g.tensor

    def tt(out, a, b, o, reads, writes):
        op("v", lambda: V.tensor_tensor(out, a, b, o), reads, writes)

    def ts(out, a, s1, s2, o, reads, writes):
        if len(o) == 1:
            op("v", lambda: V.tensor_scalar(out, a, s1, None, o[0]), reads, writes)
        else:
            op("v", lambda: V.tensor_scalar(out, a, s1, s2, o[0], o[1]), reads, writes)

    def cp(out, a, reads, writes):
        op("v", lambda: V.tensor_copy(out, a), reads, writes)

    def act(out, a, reads, writes, scale=1.0, accum=None):
        op("a", lambda: S.activation(out, a, COPY, scale=scale, accum_out=accum), reads, writes)

    def quant(q, s, a, reads, writes):
        op("v", lambda: V.quantize_mx(q, s, a), reads, writes)

    def mm(out, lq, ls, rq, rs, reads, writes):
        op("t", lambda: P.matmul_mx(out, lq, ls, rq, rs, True, True), reads, writes)

    for t in range(ROUNDS):
        wrote["qp%d" % t] = ("rq%d" % t, 2 * nmask)
        wrote["la%d" % t] = ("rl%d" % t, nmask)

    lo, hi = 4 * 16, 4 * (16 + C)
    dma("s", T.xt0[:, lo:hi], T.x[:], "dx", [], [])
    dma("a", T.ut[:], T.u[:], "du", [], ["ut"])
    dma("s", T.xt0[:, 0:lo], T.x[:, 0:lo], "dx", [], [])
    dma("s", T.xt0[:, hi:hi + lo], T.x[:, 0:lo], "dx", [], ["xt"])
    for r in range(16):
        dma("a", T.pb[r:128:16, :], T.p[:], "dpb", [], [])
    wrote["pb"] = ("dpb", count["dpb"])
    dma("s", T.pin[:], T.p[:], "dp", [], ["pin"])
    dma("s", T.wq[:].bitcast(dt.uint8), T.wc[:], "dw", [], [])
    dma("s", T.wp[:], T.ws[:], "dw", [], ["w"])
    dma("s", T.vt[:], T.v[:], "dv", [], ["vt"])

    def iota(out, pattern, base, mul, key):
        op("gc_", lambda: g.iota(out, pattern, base, mul, allow_small_or_imprecise_dtypes=True), [], [key])

    op("v", lambda: V.memset(T.eo[:], 1.0), [], ["eo"])
    for name, k, w in (("gb", 0, 16), ("gb", C + 16, 16), ("wb", C - 16, 16), ("wb", 2 * C, 16), ("ka", 20, 12), ("kb", 20, 12)):
        op("v", lambda: V.memset(T[name][:, k:k + w], 0.0), [], ["%s_pad%d" % (name, k)])
    wrote["gb_pad"], wrote["wb"] = wrote["gb_pad%d" % (C + 16)], wrote["wb_pad%d" % (2 * C)]
    iota(T.c8[:], [[16, 8]], 0, 0, "c8")
    iota(T.pi[:], [[1, 1]], 0, 1, "pi")
    iota(T.ci[:], [[1, NC]], 0, 0, "ci")
    iota(T.j16[:], [[0, NC], [1, 16]], 0, 0, "j16")
    op("gc_", lambda: g.affine_select(T.ee[:], T.eo[:], [[1, 516]], A.is_equal, 0.0, -3, -4), ["eo"], ["ee"])
    iota(T.iof[:], [[1, C]], 0, 0, "iof")
    cp(T.ul[:], T.c8[:], ["c8"], ["ul"])
    ts(T.qi[:], T.pi[:], 15, None, [A.bitwise_and], ["pi"], ["qi"])
    ts(T.oi[:], T.pi[:], 16, 4, [A.bitwise_and, A.arith_shift_right], ["pi"], ["oi"])
    cp(T.exl[:], T.ci[:], ["ci"], ["exl"])
    cp(T.qf[:], T.qi[:], ["qi"], ["qf"])
    tt(T.si[:], T.qi[:], T.oi[:], A.add, ["qi", "oi"], ["si"])
    ts(T.k2[:], T.qi[:], 16.0, None, [A.mult], ["qi"], ["k2"])
    ts(T.q20[:], T.qf[:], 20.0, None, [A.mult], ["qf"], ["q20"])
    ts(T.ri[:], T.si[:], 1, None, [A.bitwise_and], ["si"], ["ri"])
    ts(T.iw[:], T.ci[:], 16.0, T.qf[:, 0:1], [A.mult, A.add], ["ci", "qf"], ["iw"])
    ts(T.k1[:], T.ri[:], float(C + 16), None, [A.mult], ["ri"], ["k1"])
    ts(T.pbf[:], T.ci[:], T.q20[:, 0:1], None, [A.add], ["ci", "q20"], ["pbf"])
    tt(T.k3[:], T.k1[:], T.k2[:], A.add, ["k1", "k2"], ["k3"])
    cp(T.ka[:, 0:NC], T.iw[:], ["iw"], ["ka"])
    cp(T.pbl[:], T.pbf[:], ["pbf"], ["pbl"])
    cp(T.wl[:, 0:1], T.k3[:], ["k3"], ["wl0"])
    ts(T.wl[:, 1:2], T.k3[:], 256.0, float(C + E - 1), [A.add, A.min], ["k3"], ["wl1"])
    ts(T.kk[:], T.j16[:], T.qf[:, 0:1], None, [A.is_gt], ["j16", "qf"], ["kk"])

    quant(T.uq[:], T.us[:], T.ut[:], ["ut"], ["uq"])
    op("v", lambda: V.tensor_copy(T.uqr[:, 0:128].bitcast(dt.uint32), T.uq[:, 0:128].bitcast(dt.uint32).indirect(T.ul[:, 0:8])), ["uq", "ul"], ["uqr"])
    op("v", lambda: V.tensor_copy(T.usr[:, 0:128], T.us[:, 0:128].indirect(T.ul[:, 0:8])), ["uq", "ul"], ["usr"])
    for b in range(4):
        quant(T.eq[:, 128 * b:128 * b + 128], T.es[:, 128 * b:128 * b + 128], T.ee[:, 3 - b:515 - b], ["ee"], ["eq%d" % b])

    def turn(at, in_, keys, key):
        w = in_.shape[1]
        op("v", lambda: V.transpose(T.tt[:, at:at + w], in_), keys, [key])

    turned = T.tt[:].indirect(T.wl[:])
    wlk = ["wl0", "wl1"]

    for t in range(ROUNDS):
        xt = T.xt0 if t == 0 else T.xt1
        qx, sx, qk = T["qx%d" % t], T["sx%d" % t], ["qx%d_0" % t, "qx%d_1" % t]
        if t == 0:
            quant(qx[:, 0:16 + M], sx[:, 0:16 + M], xt[:, 0:lo + 4 * M], ["xt"], qk[:1])
            quant(qx[:, 16 + M:E], sx[:, 16 + M:E], xt[:, lo + 4 * M:4 * E], ["xt"], qk[1:])
        else:
            quant(qx[:, 0:16 + M], sx[:, 0:16 + M], xt[:, 0:lo + 4 * M], ["x%d_0" % b for b in range(4)] + ["xpad0"], qk[:1])
            ts(xt[:, lo + 4 * M + 3:hi:4], T.uu[:, 3 * C + M:4 * C], 2.0 ** -5, None, [A.mult], ["uu3_1"], ["x3_1"])
            quant(qx[:, 16 + M:E], sx[:, 16 + M:E], xt[:, lo + 4 * M:4 * E], ["x%d_1" % b for b in range(4)] + ["xpad1"], qk[1:])
        uk = ["uqr", "usr"]
        mm(T.ps6[:, 0:16 + M], T.uqr[:], T.usr[:], qx[:, 0:16 + M], sx[:, 0:16 + M], uk + qk[:1], ["ps6"])
        mm(T.ps0[:, 0:M], T.uqr[:], T.usr[:], qx[:, 16:16 + M], sx[:, 16:16 + M], uk + qk[:1], ["ps0"])
        mm(T.ps7[:, 0:32 + M], T.uqr[:], T.usr[:], qx[:, M:E], sx[:, M:E], uk + qk, ["ps7"])
        mm(T.ps5[:, 0:M], T.uqr[:], T.usr[:], qx[:, 16 + M:16 + C], sx[:, 16 + M:16 + C], uk + qk[1:], ["ps5"])
        send(T["qp%d" % t][:].bitcast(dt.uint8), qx[:, 16:16 + C].bitcast(dt.uint8), "rq%d" % t, "lq%d" % t, qk)
        send(T["sp%d" % t][:], sx[:, 16:16 + C], "rq%d" % t, "lq%d" % t, qk)
        act(T.nb[:, 0:M], T.ps0[:, 0:M], ["ps0"], ["nb0"])
        act(T.nb[:, M:C], T.ps5[:, 0:M], ["ps5"], ["nb1"])
        if t == 0:
            iota(T.iog[:], [[1, C]], C, 0, "iog")
            cp(T.l50[:], T.pb[:].indirect(T.pbl[:]), ["pb", "pbl"], ["l50"])
        turn(0, T.ps6[:, 16:16 + M], ["ps6"], "ta0")
        turn(C, T.ps6[:, 0:M], ["ps6"], "tb0")
        turn(M, T.ps7[:, 16:16 + M], ["ps7"], "ta1")
        turn(C + M, T.ps7[:, 0:32 + M], ["ps7"], "tb1")
        tk = ["ta0", "tb0", "ta1", "tb1"]
        cp(T.sw[:], turned, tk + wlk, ["sw"])
        sk = ["nb0", "nb1", "sw"]
        lw, ln, lk = T["lw%d" % t], T["lw%d" % (t + 1)], "lw%d" % t
        for c in range(NC):
            f, e, sc = C * c, 16 * c + 16, T.sw[:, c:c + 1]
            fk = ["fl%d" % c, "fh%d" % c]
            ts(T.fb[:, f:f + e], T.nb[:, 0:e], sc, None, [A.is_ge], sk, fk[:1])
            if e < C:
                ts(T.fb[:, f + e:f + C], T.nb[:, e:C], sc, None, [A.is_gt], sk, fk[1:])
            if c == NC - 1:
                op("v", lambda: V.tensor_reduce(T.acc[:, c:c + 1], T.fb[:, f:f + C], AxisListType.X, A.add), fk, ["acc%d" % c])
            else:
                act(T.fb[:, f:f + C], T.fb[:, f:f + C], fk, fk + ["acc%d" % c], accum=T.acc[:, c:c + 1])
            if c == 4:
                act(T.ex[:], T.sw[:].indirect(T.exl[:]), ["sw", "exl"], ["ex"])
            if c == 8 and t == 0:
                cp(T.lw0[:], T.pin[:], ["pin"], ["lw0"])
                ts(T.iov[:], T.iof[:], float(-M), 2.0 ** -9, [A.add, A.mult], ["iof"], ["iov"])
            if c == 10 and t == 0:
                tt(T.vb[:], T.l50[:], T.iov[:], A.add, ["l50", "iov"], ["vb"])
            if c == 15:
                ts(T.kb[:, 0:NC], lw[:], float(-M), 2.0 ** -9, [A.add, A.mult], [lk], ["kb"])
                tt(T.f1[:], lw[:], T.iw[:], A.subtract, [lk, "iw"], ["f1"])
            if c == 16:
                tt(T.te[:, 0:M], T.ps0[:, 0:M], T.ex[:, 0:M], A.is_equal, ["ps0", "ex"], ["te0"])
                tt(T.te[:, M:C], T.ps5[:, 0:M], T.ex[:, M:C], A.is_equal, ["ps5", "ex"], ["te1"])
            if c == 17:
                op("v", lambda: V.tensor_tensor_scan(T.ts[:], T.te[:], T.kk[:], 0.0, A.add, A.mult), ["te0", "te1", "kk"], ["ts"])
        for dst, w, key in ((T.hw, 2 * C, "h"), (T.hx, C, "g")):
            for b in range(4):
                if t == 0:
                    act(dst[:, w * b:w * b + C], T.xt0[:, lo + b:hi:4], ["xt"], [key + str(b)], scale=0.5)
                else:
                    act(dst[:, w * b:w * b + C], T.uu[:, C * b:C * b + C], ["uu%d_0" % b, "uu%d_1" % b], [key + str(b)], scale=2.0 ** -6)
        for b in range(4):
            k = "ps%d" % (1 + b)
            mm(T[k][:, 0:C], T.eq[:, 128 * b:128 * b + 128], T.es[:, 128 * b:128 * b + 128], T["qp%d" % t][:], T["sp%d" % t][:], ["eq%d" % b, "qp%d" % t], [k])
            act(T.hw[:, 2 * C * b + C:2 * C * b + 2 * C], T[k][:, 0:C], [k], ["d%d" % b], scale=0.5)
        if t == 0:
            for i, k in enumerate((0, hi)):
                act(T.xt1[:, k:k + lo], T.xt0[:, k:k + lo], ["xt"], ["xpad%d" % i])
        tt(T.pli[:], T.acc[:], T.ts[:, 15:C:16], A.subtract, ["acc%d" % c for c in range(NC)] + ["ts"], ["pli"])
        ts(T.hh[:], T.pli[:], -1.5, 0.5, [A.add, A.mult], ["pli"], ["hh"])
        ts(T.pq[:], T.pli[:], 0.25, None, [A.mult], ["pli"], ["pq"])
        ts(T.plu[:], T.pli[:], -1.0, None, [A.add], ["pli"], ["plu"])
        tt(T.pxi[:], T.hh[:], T.pq[:], A.subtract, ["hh", "pq"], ["pxi"])
        cp(T.wo[:].indirect(T.plu[:]), T.vb[:], ["plu", "vb"], ["wo"])
        ts(T.pxu[:], T.pxi[:], 4.0, 2.0, [A.mult, A.add], ["pxi"], ["pxu"])
        cp(T.gb[:, 16:16 + C], T.wo[:].indirect(T.pxu[:]), ["wo", "pxu"], ["gb"])
        turn(0, T.gb[:, 16:16 + C], ["gb", "ta1"], "ta0")
        turn(C, T.gb[:], ["gb", "gb_pad", "tb1"], "tb0")
        cp(T.bl[:], turned, ["ta0", "tb0"] + wlk, ["bl"])
        tt(T.qb[:], turned, T.kb[:], A.subtract, ["ta0", "tb0", "kb", "kb_pad20"] + wlk, ["qb"])
        tt(T.qa[:], turned, T.ka[:], A.subtract, ["ta0", "tb0", "ka", "ka_pad20"] + wlk, ["qa"])
        tt(T.xb[:], T.bl[:, 0:NC], T.qb[:, 0:NC], A.subtract, ["bl", "qb"], ["xb"])
        ts(T.ca[:], T.qa[:, 0:NC], -0.4, C - 0.6, [A.max, A.min], ["qa"], ["ca"])
        tt(T.dl[:], T.bl[:, 0:NC], lw[:], A.subtract, ["bl", lk], ["dl"])
        ts(T.cb[:], T.xb[:], 0.0, (C - 1) / 512.0, [A.max, A.min], ["xb"], ["cb"])
        tt(T.oa[:], T.ca[:], T.qa[:, 0:NC], A.is_equal, ["ca", "qa"], ["oa"])
        ts(T.e5[:], T.xb[:], -512.0, None, [A.mult], ["xb"], ["e5"])
        tt(T.ob[:], T.cb[:], T.xb[:], A.is_equal, ["cb", "xb"], ["ob"])
        tt(T.m1[:], T.oa[:], T.dl[:], A.mult, ["oa", "dl"], ["m1"])
        tt(T.db[:], T.f1[:], T.e5[:], A.add, ["f1", "e5"], ["db"])
        tt(T.md[:], T.m1[:], T.ob[:], A.mult, ["m1", "ob"], ["md"])
        tt(T.mm[:], T.oa[:], T.ob[:], A.mult, ["oa", "ob"], ["mm"])
        tt(ln[:], lw[:], T.md[:], A.add, [lk, "md"], ["lw%d" % (t + 1)])
        tt(T.pm[:], T.mm[:], T.db[:], A.mult, ["mm", "db"], ["pm"])
        lu, luk = T["lu%d" % t], "lu%d" % t
        cp(lu[:], ln[:], ["lw%d" % (t + 1)], [luk])
        send(T["la%d" % t][:], lu[:], "rl%d" % t, "ll%d" % t, [luk])
        tt(T.pf[:], T.pm[:], T.iw[:], A.add, ["pm", "iw"], ["pf"])
        cp(T.wb[:, C:3 * C].indirect(lu[:]), T.iof[:], [luk, "iof"], ["wb"])
        cp(T.pu[:], T.pf[:], ["pf"], ["pu"])
        l5, l5k = T["l5%d" % t], "l5%d" % t
        if t + 1 < ROUNDS:
            act(T["l5%d" % (t + 1)][:], l5[:].indirect(T.pu[:]), [l5k, "pu"], ["l5%d" % (t + 1)])
            tt(T.vb[:], l5[:].indirect(T.pu[:]), T.iov[:], A.add, [l5k, "pu", "iov"], ["vb"])
        else:
            act(T.olb[:], l5[:].indirect(T.pu[:]), [l5k, "pu"], ["olb"])
            dma("s", T.ol[:], T.olb[0:128:16, :], "dol", ["olb"], [])
            quant(T.vq[:], T.vs[:], T.vt[:], ["vt"], ["vq"])
        cp(T.wb[:, 0:2 * C].indirect(T["la%d" % t][:]), T.iog[:], ["la%d" % t, "iog"], ["wb"])
        turn(0, T.wb[:, C:2 * C], ["wb"], "ta0")
        turn(C, T.wb[:, C - 16:2 * C + 16], ["wb"], "tb0")
        cp(T.eu[:], turned, ["ta0", "tb0"] + wlk, ["eu"])
        for b, h, n in ((0, 0, 2), (1, 0, 2), (2, 0, 2), (3, 0, 1), (3, 1, 1)):
            o, j, w = 2 * C * b, M * h, M * n
            zk = ["z%d_%d" % (b, i) for i in range(h, h + n)]
            tt(T.z[:, 4 * j + b:4 * (j + w):4], T.hw[:, o:o + 2 * C].indirect(T.eu[:, j // 16:(j + w) // 16]), T.hx[:, C * b + j:C * b + j + w], A.add,
               ["eu", "h%d" % b, "g%d" % b, "d%d" % b], zk)
            act(T.z32[:, C * b + j:C * b + j + w], T.z[:, 4 * j + b:4 * (j + w):4], zk, ["zz%d_%d" % (b, i) for i in range(h, h + n)], scale=32.0)
        banks = (("ps6", "ps7", "ps1", "ps2"), ("ps3", "ps4", "ps0", "ps5"))
        for h in range(2):
            j = M * h
            quant(T.zq[:, j:j + M], T.zs[:, j:j + M], T.z[:, 4 * j:4 * (j + M)], ["z%d_%d" % (b, h) for b in range(4)], ["zq%d" % h])
            for b in range(4):
                k = banks[h][b]
                mm(T[k][:, 0:M], T.wq[:, 128 * b:128 * b + 128], T.wp[:, 128 * b:128 * b + 128], T.zq[:, j:j + M], T.zs[:, j:j + M], ["w", "zq%d" % h], [k])
        for h in range(2):
            j = M * h
            for b in range(4):
                k, u = banks[h][b], T.uu[:, C * b + j:C * b + j + M]
                tt(u, T[k][:, 0:M], T.z32[:, C * b + j:C * b + j + M], A.add, [k, "zz%d_%d" % (b, h)], ["uu%d_%d" % (b, h)])
                if b < 3:
                    act(T.xt1[:, lo + 4 * j + b:lo + 4 * (j + M):4], u, ["uu%d_%d" % (b, h)], ["x%d_%d" % (b, h)], scale=2.0 ** -5)
                if (b, h) == (0, 1):
                    ts(T.xt1[:, lo + 3:lo + 4 * M:4], T.uu[:, 3 * C:3 * C + M], 2.0 ** -5, None, [A.mult], ["uu3_0"], ["x3_0"])

    q3, s3 = T["qx%d" % ROUNDS], T["sx%d" % ROUNDS]
    for h in range(2):
        j, k = M * h, ("ps6", "ps7")[h]
        if h:
            ts(T.xt1[:, lo + 4 * M + 3:hi:4], T.uu[:, 3 * C + M:4 * C], 2.0 ** -5, None, [A.mult], ["uu3_1"], ["x3_1"])
        quant(q3[:, j:j + M], s3[:, j:j + M], T.xt1[:, lo + 4 * j:lo + 4 * (j + M)], ["x%d_%d" % (b, h) for b in range(4)], ["q3_%d" % h])
        mm(T[k][:, 0:M], T.vq[:], T.vs[:], q3[:, j:j + M], s3[:, j:j + M], ["vq", "q3_%d" % h], [k])
    for h in range(2):
        j, k = M * h, ("ps6", "ps7")[h]
        cp(T.yb[:, j:j + M], T[k][:, 0:M], [k], ["yb%d" % h])
        dma("as"[h], T.y[:, j:j + M], T.yb[:, j:j + M], "dy", ["yb%d" % h], [])
    qk = ["q3_0", "q3_1"]
    dma("a", T.oc[:], q3[:].bitcast(dt.uint8), "doc", qk, [])
    for k in range(4):
        dma("s" if k % 2 else "a", T.osc[4 * k:4 * k + 4, :], s3[32 * k:32 * k + 4, :], "doc", qk, [])
    for t in range(ROUNDS):
        count["rq%d" % t], count["rl%d" % t] = 2 * nmask, nmask
    need("s", [(s, m) for s, m in count.items()])
